import numpy as np, ml_dtypes
CORES = [40,64,80,88,96,104,120,144]
N = 8
import mx_ref
BF = ml_dtypes.bfloat16
def gentries(a):
    return np.ascontiguousarray(a.reshape(8, 16, -1).transpose(0, 2, 1)).reshape(8, -1)
def gtable(e):
    e = np.asarray(e); return np.ascontiguousarray(e.reshape(8, -1, 16).transpose(0, 2, 1)).reshape(128, -1).astype(np.int32)
def gcols(t, e):
    v = np.concatenate([t.reshape(8, 16, -1, 4), np.zeros((8, 16, 1, 4), BF)], axis=2)
    return np.ascontiguousarray(np.stack([v[g][:, e[g]] for g in range(8)])).reshape(128, -1)
def tile(rs):
    return np.stack(rs, axis=2).reshape(128, -1).astype(BF)
def cut(t, i, w=512):
    return t[:, w * i:w * i + w]
def pick(q, e):
    c = np.concatenate([q[0].reshape(128, -1, 4), np.zeros((128, 1, 4), np.uint8)], axis=1); s = np.concatenate([q[1], np.ones((16, 1), np.uint8)], axis=1)
    return (np.ascontiguousarray(c[:, e].reshape(128, -1)), np.ascontiguousarray(s[:, e]))
def join(*qs):
    return (np.concatenate([q[0] for q in qs], axis=1), np.concatenate([q[1] for q in qs], axis=1))
def put(q, e, v):
    c, s = q[0].reshape(128, -1, 4).copy(), q[1].copy(); c[:, e] = v[0].reshape(128, -1, 4); s[:, e] = v[1]
    return (c.reshape(128, -1), s)
def pk(c, s):
    return (np.ascontiguousarray(c), mx_ref.live(s))
def emit(q):
    return q[0], q[1]
def packed(v, rng):
    q = [mx_ref.quantize(np.ascontiguousarray(v[r])) for r in range(N)]
    return np.stack([a for a, b in q]), np.stack([mx_ref.plane(b, rng) for a, b in q])
def values_of_codes():
    e, c = np.zeros((128, 128, 4), np.float32), np.zeros((128, 2, 4), np.uint8)
    e[np.arange(128), np.arange(128), 0] = 1
    c[:127, :, 0] = np.arange(256).reshape(2, 128).T[:127]
    return mx_ref.matmul(mx_ref.quantize(e.reshape(128, 512).astype(BF)), (c.reshape(128, 8), np.full((16, 2), 127, np.uint8))).T.reshape(-1).astype(np.float64)
CODE_VALUE, SCALE_VALUE = values_of_codes(), 2.0 ** (np.arange(256) - 127.0)
def decode(q):
    return (CODE_VALUE[q[0]].reshape(16, 8, -1, 4) * SCALE_VALUE[q[1]][:, None, :, None] + 0.0).reshape(128, -1).astype(np.float32)
def f(rng, *shape):
    return mx_ref.flush((rng.standard_normal(shape, dtype=np.float32) * np.exp2(rng.integers(-2, 3, shape[:-1] + (1,)))).astype(BF))
def wide(rng, *shape, cols=0):
    v = rng.standard_normal(shape, dtype=np.float32) * np.exp2(rng.integers(-12, 13, shape)).astype(np.float32)
    if cols: v *= np.repeat(np.exp2(rng.integers(-cols, cols + 1, shape[:-2] + (1, shape[-1] // 4))) * (rng.random(shape[:-2] + (1, shape[-1] // 4)) > 0.0625), 4, axis=-1).astype(np.float32)
    return mx_ref.flush(v.astype(BF))
C, K, M, R, S = 320, 64, 3, 3, 4
def order(p):
    return np.argsort(-(p[::16] + np.float32(0.0)), axis=1, kind="stable")
def replies(o, m):
    place = np.argsort(o, axis=1)
    label = np.where(place >= C - K, 2, 0)
    when = np.zeros((8, C), int)
    for n in range(1, S + 1):
        to = np.take_along_axis(label, m, axis=1).reshape(8, M, C)
        won = (label == 0) & (to == 2).any(axis=1)
        lost = (label == 0) & (to == 1).all(axis=1)
        when[won | lost] = n
        label[won] = 1
        label[lost] = 2
    to = np.take_along_axis(label, m, axis=1).reshape(8, M, C)
    at = np.take_along_axis(when, m, axis=1).reshape(8, M, C)
    best = np.argmin(np.take_along_axis(place, m, axis=1).reshape(8, M, C), axis=1)
    k = np.where(label == 1, np.argmin(np.where(to == 2, at, S + 1), axis=1), np.where(label == 2, np.argmax(np.where(to == 1, at, -1), axis=1), best))
    t = np.take_along_axis(m.reshape(8, M, C), k[:, None], axis=1)[:, 0]
    return np.concatenate([np.where(place >= C - K, place + K, t), np.tile(C + np.arange(K), (8, 1))], axis=1)
def big(v):
    v = v.astype(np.float32)
    v[np.abs(v) < np.float32(2.0 ** -16)] = 0
    return v.astype(BF)
def numbers_of(rng):
    return {"x": big(f(rng, N, 128, 4 * C)), "u": np.array(f(rng, N, 128, 512)), "v": np.array(f(rng, N, 128, 512))}
def moves(rng):
    return np.stack([gtable(rng.integers(0, C, (8, M * C))) for r in range(N)])
def weights(rng, w):
    c, p = packed(w, rng)
    return {"wc": c, "ws": p}
def within(rng, a, b):
    w = np.array(f(rng, N, 128, 2048)).reshape(N, 8, 16, 4, 8, 16, 4)
    z = np.zeros_like(w)
    z[:, :, a:b, :, :, a:b] = w[:, :, a:b, :, :, a:b]
    return weights(rng, z.reshape(N, 128, 2048))
def signs(rng):
    return np.stack([rng.permutation(8) % 2 * 2.0 - 1.0 for r in range(N)])
def lead(rng, m, i, one, others):
    m[:, i] = rng.choice(others, (M, len(i)))
    m[rng.integers(0, M, len(i)), i] = rng.choice(one, len(i))
def game(rng, dead, rest, kind, g):
    m = rng.integers(0, C, (M, C))
    a, b, c, d, e, h = np.array_split(rng.permutation(rest), 6)
    if kind == 0:
        lead(rng, m, a, dead, np.arange(C))
        lead(rng, m, b, a, a)
        lead(rng, m, c, b, rest)
        lead(rng, m, d, c, np.concatenate([a, c]))
        lead(rng, m, e, d, np.concatenate([a, c, d, e]))
        lead(rng, m, h, h, np.concatenate([a, c, h]))
    elif kind == 1:
        lead(rng, m, rest, rest, rest)
        z = np.sort(rest[:C - 2 * K])[-2:]
        i = rng.choice(rest, 8)
        m[0, i] = z[1]
        m[1:, i] = z[0]
    elif kind == 2 and g % 2: lead(rng, m, rest, dead, np.arange(C))
    elif kind == 2: m[:] = dead[0]
    else:
        lead(rng, m, a, dead, np.arange(C))
        lead(rng, m, np.concatenate([b, c, d, e, h]), a, a)
    return m
def setup_inputs(rng):
    return {**numbers_of(rng), "mv": moves(rng), **weights(rng, f(rng, N, 128, 2048))}
def setup_inputs_ties(rng):
    d = numbers_of(rng)
    e = rng.permutation(N)
    x = d["x"].reshape(N, 8, 16, C, 4)
    for r in range(N):
        k = np.zeros(C, int) if r == e[0] else rng.permutation(C) % 3
        a = x[r][:, :8, :3].copy()
        a[:, :, 2] = 0
        x[r][:, :8] = a[:, :, k]
    x[e[1]] = 0
    u = d["u"].reshape(N, 8, 16, 128, 4)
    u[:, :, 8:, ::16] = 0
    w = np.array(f(rng, N, 128, 2048)).reshape(N, 8, 16, 4, 8, 16, 4)
    w[:, :, 8:, :, :, :8] = 0
    return {"x": x.reshape(N, 128, 4 * C), "u": u.reshape(N, 128, 512), "v": d["v"], "mv": moves(rng), **weights(rng, w.reshape(N, 128, 2048))}
def setup_inputs_near(rng):
    d = numbers_of(rng)
    x = d["x"].astype(np.float32).reshape(N, 8, 16, C, 4)
    s = np.arange(C) // 2
    g = ((s[:, None] >> np.arange(8)) & 1) * np.exp2(np.arange(8) - 23.0)
    c = np.stack([rng.permutation(8) for r in range(N)])
    z = c % 2 * 2.0 - 1.0
    x[:, :, 0] = 0
    x[:, :, 0, :, 0] = z[:, :, None]
    j = rng.integers(0, C, N)
    x[np.arange(N)[:, None], np.arange(8), 0, j[:, None], 0] = np.where(z > 0, 2.0 ** 30, np.where(c % 4 == 0, -2.0 ** 30, -1.0))
    x[:, :, 8] = g[:, :4]
    x[:, :, 9] = g[:, 4:]
    x[:, :, 10:] = rng.integers(4, 8, (N, 8, 6, C, 4)) * rng.choice([-1.0, 1.0], (N, 8, 6, C, 4)) * 2.0 ** -20
    u = d["u"].reshape(N, 128, 128, 4)
    k = np.where(rng.permutation(N) < N // 2, 2.0 ** -30, 1.0).astype(np.float32).astype(BF)
    u[:, :, ::16] = 0
    for h in range(0, 128, 16):
        u[:, h, h, 0] = k
        u[:, h + 8:h + 10, h] = k[:, None, None]
    return {"x": x.reshape(N, 128, 4 * C).astype(BF), "u": u.reshape(N, 128, 512), "v": d["v"], "mv": moves(rng), **within(rng, 1, 8)}
def setup_inputs_waves(rng):
    d = numbers_of(rng)
    o = rng.permutation(N)
    small = rng.permutation(N) < N // 2
    c = np.zeros((N, 8, C))
    m = []
    for r in range(N):
        own = []
        for g in range(8):
            e = rng.permutation(C)
            c[r, g, e[:K]] = -1
            c[r, g, e[C - K:]] = 1
            own.append(game(rng, e[:K], e[K:], o[r] % 4, g).reshape(-1))
        m.append(gtable(np.stack(own)))
    k = np.where(small, 2.0 ** -30, 1.0).astype(np.float32)
    x = d["x"].reshape(N, 8, 16, C, 4)
    x[:, :, :8] = 0
    x[:, :, 0, :, 0] = ((2.5 * np.abs(c) + 0.5 * c) * k[:, None, None]).astype(np.float32).astype(BF)
    x[:, :, 1, :, 0] = ((2.5 * np.abs(c) - 0.5 * c) * k[:, None, None]).astype(np.float32).astype(BF)
    u = d["u"].reshape(N, 128, 128, 4)
    u[:, :, ::16] = 0
    for h in range(0, 128, 16):
        u[:, h, h, 0] = k.astype(BF)
        u[:, h + 1, h, 0] = (-k).astype(BF)
    return {"x": x.reshape(N, 128, 4 * C), "u": u.reshape(N, 128, 512), "v": d["v"], "mv": np.stack(m), **within(rng, 8, 16)}
def setup_inputs_huge(rng):
    d = numbers_of(rng)
    x = 2.0 ** 29 * (0.8 + 0.2 * rng.random((N, 128, C, 4)))
    c = np.stack([rng.permutation(C) % 2 * 2.0 - 1.0 for r in range(N)])
    c[rng.permutation(N) < N // 2] = 1
    x *= c[:, None, :, None]
    u = d["u"].reshape(N, 128, 128, 4)
    a = 2.0 ** 30 * (1 - 0.25 * rng.random((N, 128, 8, 4))) * signs(rng)[:, None, :, None]
    u[:, :, ::16] = a.astype(np.float32).astype(BF)
    w = np.zeros((N, 128, 4, 128, 4), np.float32)
    i = np.arange(128)
    for b in range(4): w[:, i, b, i, b] = 4
    return {"x": x.astype(np.float32).reshape(N, 128, 4 * C).astype(BF), "u": u.reshape(N, 128, 512), "v": d["v"], "mv": moves(rng), **weights(rng, w.reshape(N, 128, 2048).astype(BF))}
def setup_inputs_spread(rng):
    d = setup_inputs(rng)
    d["x"] = big(wide(rng, N, 128, 4 * C, cols=6))
    return d
def check_inputs(d):
    b = []
    for k in ("x", "u", "v"):
        a = np.abs(d[k].astype(np.float32))
        if not (np.isfinite(a).all() and ((a == 0) | (a >= 2.0 ** -30) & (a <= 2.0 ** 30)).all()): b.append("a value of " + k)
    if ((d["mv"] < 0) | (d["mv"] >= C)).any(): b.append("an entry of mv")
    if (d["wc"] % 128 == 127).any(): b.append("a code of wc")
    none, low, high = [np.max(s) for c, s in [mx_ref.quantize(np.full((128, 16), k).astype(BF)) for k in (0.0, 2.0 ** -30, 2.0 ** 30)]]
    live = np.stack([mx_ref.live(p) for p in d["ws"]])
    if ((live != none) & ((live < low) | (live > high))).any(): b.append("a scale of ws")
    return b
def reference(x, u, v, mv, wc, ws):
    qu = [mx_ref.quantize(u[r]) for r in range(N)]
    lay = [pk(wc[r], ws[r]) for r in range(N)]
    now = [x[r] for r in range(N)]
    to = [None] * N
    for n in range(R):
        border = []
        for r in range(N):
            o = order(mx_ref.matmul(qu[r], mx_ref.quantize(now[r])))
            border.append(mx_ref.quantize(gcols(now[r], o[:, :K])))
            to[r] = replies(o, gentries(mv[r]))
        came = decode(join(*border)).astype(BF)
        for r in range(N):
            both = np.concatenate([now[r], cut(came, (r + 1) % N, 4 * K)], axis=1)
            t = to[r][:, :C]
            one = gcols(both, t).astype(np.float32)
            two = gcols(both, np.take_along_axis(to[r], t, axis=1)).astype(np.float32)
            q = mx_ref.quantize(((one + two) * np.float32(0.5)).astype(BF))
            old = now[r].astype(np.float32)
            now[r] = tile([old[:, b::4] + mx_ref.matmul(pick(lay[r], np.arange(128 * b, 128 * b + 128)), q) * np.float32(0.03125) for b in range(4)])
    y, ot = np.zeros((N, 128, C), np.float32), np.zeros((N, 8, C), np.float32)
    oc, osc = np.zeros((N, 128, 4 * C), np.uint8), np.zeros((N, 16, C), np.uint8)
    for r in range(N):
        q = mx_ref.quantize(now[r])
        y[r] = mx_ref.matmul(mx_ref.quantize(v[r]), q)
        ot[r] = to[r][:, :C]
        oc[r], osc[r] = emit(q)
    return {"y": y, "ot": ot, "oc": oc, "osc": osc}

@@ -1,0 +1,564 @@
+from concourse.mybir import dt, AluOpType, ActivationFunctionType
+
+C, K, R = 320, 64, 3
+HC = C // 2
+FW = C + K
+BB = 524288.0
+AL = -0.375 * BB
+OFF = 262144.0
+HUGE = 2.0 ** 80
+ACT_ROWS = 9
+
+F32, BF, I32, U16, MX, U8 = "float32", "bfloat16", "int32", "uint16", "float8_e4m3fn_x4", "uint8"
+
+
+def _sb(n, d):
+    return ("sbuf", [128, n], d)
+
+
+SCRATCH = {
+    "xt": _sb(4 * C, BF), "xn": _sb(4 * C, BF), "ut": _sb(512, BF), "vt": _sb(512, BF),
+    "qu": _sb(128, MX), "su": _sb(128, U8), "qp": _sb(128, MX), "sp": _sb(128, U8),
+    "qv": _sb(128, MX), "sv": _sb(128, U8), "qx": _sb(C, MX), "sx": _sb(C, U8),
+    "qw": _sb(512, MX), "sw": _sb(512, U8), "qz": _sb(C, MX), "sz": _sb(C, U8),
+    "qk": _sb(128, MX), "sk": _sb(128, U8), "qe": _sb(512, MX), "se": _sb(512, U8),
+    "qc": _sb(6 * C, MX), "sc": _sb(6 * C, U8),
+    "qb": _sb(128 * R, MX), "sb": _sb(128 * R, U8),
+    "qr": _sb(K * R, MX), "sr": _sb(K * R, U8),
+    "ql": _sb(128 + K * R, MX), "sl": _sb(128 + K * R, U8),
+    "mvi": _sb(60, I32), "mvo": _sb(60, U16), "d2": _sb(20, F32),
+    "yy": _sb(4 * C, BF), "fx": _sb(4 * FW, BF), "hh": _sb(4 * FW, F32), "zt": _sb(4 * C, BF),
+    "bt": _sb(512, BF), "zero": _sb(512, BF), "ct": _sb(6 * 4 * C, BF), "et": _sb(520, BF),
+    "kt": _sb(512, BF), "g8": _sb(512, BF), "dec": _sb(4 * K, F32), "ys": _sb(C, F32),
+    "pi": _sb(2, I32), "qi": _sb(2, I32), "gi": _sb(2, I32), "pa": _sb(2, I32), "pb": _sb(2, I32),
+    "cols": _sb(16, F32), "sm": _sb(8, F32), "uo": _sb(8, U16), "po": _sb(4, U16), "bias": _sb(8, F32),
+    "tt": _sb(32, F32), "tr": _sb(32, F32), "to": _sb(20, U16),
+    "jr": _sb(C, I32), "jj": _sb(C, I32), "junk": _sb(5 * C, F32),
+    "gs": _sb(8, F32), "oa": _sb(4, F32), "ob": _sb(4, F32), "oo": _sb(4, U16),
+    "ta": _sb(20, F32), "tb": _sb(20, F32), "ki": _sb(20, I32), "kk": _sb(20, I32), "sg": _sb(20, F32),
+    "h0": _sb(100, F32), "h1": _sb(100, F32), "ho": _sb(100, F32),
+    "ps": ("psum", [128, 512 * 8], F32),
+}
+for _n in ("rr ii mk rs mm d1 vv key a0 a1 s1 ca cb c1 c2 c3 c4 n0 n1 n2 e1 e2 s3 s4 t1 t3 t4").split():
+    SCRATCH[_n] = _sb(C, F32)
+POOL = ["p%d" % i for i in range(110)]
+SEMAPHORES = POOL + ["arr%d" % r for r in range(R)] + ["mid%d" % r for r in range(R)] + ["sent"]
+
+A = AluOpType
+FN = ActivationFunctionType
+
+
+def V(name, a, n, step=1):
+    return (name, a, n, step)
+
+
+def bank(b, a=0, n=C):
+    return ("ps", 512 * b + a, n, 1)
+
+
+def _meet(u, v):
+    if u[0] != v[0]:
+        return False
+    if u[0] == "ps":
+        return u[1] // 512 == v[1] // 512
+    if u[1] + (u[2] - 1) * u[3] < v[1] or v[1] + (v[2] - 1) * v[3] < u[1]:
+        return False
+    return u[3] != v[3] or (u[1] - v[1]) % u[3] == 0
+
+
+def road(T, topo, r):
+    n = len(T.cores)
+    src, dst = T.cores[(r + 1) % n], T.cores[r]
+    if topo.may_write(src, dst):
+        return src, None, dst
+    able = [c for c in topo.cores_of(src) if c != src and T.rank_of(c) is None and topo.may_write(c, dst)]
+    able.sort(key=lambda c: topo.die(c) != topo.die(src))
+    return src, able[:2], dst
+
+
+def piece(T, where, part, r):
+    names, a = {"made": (("qb", "sb"), 128 * r), "mid": (("qr", "sr"), K * r), "land": (("ql", "sl"), 128 + K * r)}[where]
+    v = T[names[part]][:, a:a + K]
+    return v.bitcast(dt.uint8) if part == 0 else v
+
+
+def write(g, T, topo, me, to, out, in_, sem):
+    rid, pid = topo.addr(to, me)
+    return g.remote_dma(out, in_, T.sem[sem], T.sem.sent, pid, rid, topo.mask(me, to))
+
+
+def relay_program(g, core, T, topo, src, dst, part):
+    for r in range(R):
+        g.wait_ge(T.sem["mid%d" % r], len(topo.engines(src, core)))
+        write(g, T, topo, core, dst, piece(T, "land", part, r), piece(T, "mid", part, r), "arr%d" % r)
+    g.wait_ge(T.sem.sent, R * len(topo.engines(core, dst)))
+
+
+def run(ops, queues, T):
+    known = dict((q, 0) for q in queues)
+    members = {}
+    for i, o in enumerate(ops):
+        members.setdefault(o["grp"] if o["grp"] is not None else ("op", i), []).append(i)
+    gid = [o["grp"] if o["grp"] is not None else ("op", i) for i, o in enumerate(ops)]
+    at_issue, waits, needed = [], [], set()
+    touch = {}
+    for i, o in enumerate(ops):
+        q = o["q"]
+        deps = set(o["after"])
+        for v, w in [(v, False) for v in o["r"]] + [(v, True) for v in o["w"]]:
+            for j, u, wj in touch.get(v[0], []):
+                if known[q] >> j & 1 or not _meet(u, v):
+                    continue
+                if v[0] == "ps" and not w and not wj and ops[j]["q"] == q:
+                    continue
+                if w or wj or v[0] == "ps":
+                    if not (o["acc"] and gid[j] == gid[i]):
+                        deps.add(j)
+        mine = []
+        for j in sorted(deps, reverse=True):
+            if known[q] >> j & 1:
+                continue
+            assert members[gid[j]][-1] < i, (o["name"], ops[j]["name"])
+            mine.append(gid[j])
+            needed.add(gid[j])
+            for k in members[gid[j]]:
+                known[q] |= (1 << k) | at_issue[k]
+        waits.append(mine)
+        at_issue.append(known[q])
+        for v in o["r"]:
+            touch.setdefault(v[0], []).append((i, v, False))
+        for v in o["w"]:
+            touch.setdefault(v[0], []).append((i, v, True))
+    count = dict((s, 0) for s in POOL)
+    users = dict((s, 0) for s in POOL)
+    sem_of = {}
+    for i, o in enumerate(ops):
+        eng = queues[o["q"]]
+        for gk in waits[i]:
+            s, n = sem_of[gk]
+            eng.wait_ge(T.sem[s], n)
+        for s, n in o["ext"]:
+            eng.wait_ge(T.sem[s], n)
+        if o["fn"] is None:
+            continue
+        ins = o["fn"]()
+        gk = gid[i]
+        if gk in needed:
+            step = 16 if o["dma"] else 1
+            if gk not in sem_of:
+                free = [s for s in POOL if users[s] & ~at_issue[i] == 0 and not (o["dma"] and count[s])]
+                s = free[0]
+                count[s] += step * len(members[gk])
+                for k in members[gk]:
+                    users[s] |= 1 << k
+                if o["dma"]:
+                    users[s] |= 1 << len(ops)
+                sem_of[gk] = (s, count[s])
+            ins.then_inc(T.sem[sem_of[gk][0]], step)
+
+
+def rank_ops(g, core, T, topo, rank):
+    ops = []
+    vec, act, pe, sy = g.vector, g.scalar, g.tensor, g.sync
+
+    def ap(v):
+        if v[3] == 1:
+            return T[v[0]][:, v[1]:v[1] + v[2]]
+        return T[v[0]][:, v[1]:v[1] + (v[2] - 1) * v[3] + 1:v[3]]
+
+    def put(q, name, fn, r, w, grp=None, dma=False, acc=False, ext=(), after=()):
+        ops.append({"q": q, "name": name, "fn": fn, "r": list(r), "w": list(w), "grp": grp, "dma": dma, "acc": acc,
+                    "ext": list(ext), "after": list(after)})
+        return len(ops) - 1
+
+    def src(v, off):
+        return ap(v) if off is None else ap(v).indirect(ap(off))
+
+    def views(*xs):
+        return [x for x in xs if isinstance(x, tuple)]
+
+    def num(x):
+        return ap(x) if isinstance(x, tuple) else x
+
+    def ts(out, in0, s1, op0, s2=None, op1=None, off=None, grp=None):
+        if op1 is None:
+            fn = lambda: vec.tensor_scalar(ap(out), src(in0, off), num(s1), None, op0)
+        else:
+            fn = lambda: vec.tensor_scalar(ap(out), src(in0, off), num(s1), num(s2), op0, op1)
+        put("v", "ts " + out[0], fn, views(in0, s1, s2, off), [out], grp)
+
+    def tt(out, in0, in1, op, off=None, grp=None):
+        put("v", "tt " + out[0], lambda: vec.tensor_tensor(ap(out), src(in0, off), ap(in1), op), views(in0, in1, off), [out], grp)
+
+    def cp(out, in0, off=None, grp=None):
+        put("v", "cp " + out[0], lambda: vec.tensor_copy(ap(out), src(in0, off)), views(in0, off), [out], grp)
+
+    def scan(out, d0, d1, op0, op1):
+        put("v", "scan " + out[0], lambda: vec.tensor_tensor_scan(ap(out), ap(d0), ap(d1), 0.0, op0, op1), [d0, d1], [out])
+
+    def fill(out, c):
+        put("v", "fill " + out[0], lambda: vec.memset(ap(out), c), [], [out])
+
+    def quant(q, s, t):
+        put("v", "quant " + q[0], lambda: vec.quantize_mx(ap(q), ap(s), ap(t)), [t], [q, s])
+
+    def af(out, in0, func, scale=1.0, bias=0.0, off=None, acc=None, grp=None):
+        if acc is not None:
+            fn = lambda: act.activation(ap(out), src(in0, off), func, bias=num(bias), scale=scale, accum_out=ap(acc))
+        elif func == FN.Copy:
+            fn = lambda: act.activation(ap(out), src(in0, off), func, scale=scale)
+        else:
+            fn = lambda: act.activation(ap(out), src(in0, off), func, bias=num(bias), scale=scale)
+        put("a", "act " + out[0], fn, views(in0, bias, off), views(out, acc), grp)
+
+    def mm(out, lq, ls, rq, rs_, start=True, stop=True, grp=None, ext=()):
+        put("t", "mm", lambda: pe.matmul_mx(ap(out), ap(lq), ap(ls), ap(rq), ap(rs_), start, stop), [lq, ls, rq, rs_], [out],
+            grp, acc=not start, ext=ext)
+
+    def iota(out, pattern, base, cm, small):
+        if small:
+            fn = lambda: g.iota(ap(out), pattern, base, cm, allow_small_or_imprecise_dtypes=True)
+        else:
+            fn = lambda: g.iota(ap(out), pattern, base, cm)
+        put("g", "iota " + out[0], fn, [], [out])
+
+    stores = []
+
+    def dma(q, out, in0, r, w, grp=None):
+        eng = {"s": sy, "a": act}[q]
+        i = put(q, "dma", lambda: eng.dma_start(out(), in0()), r, w, grp, dma=True)
+        if not w:
+            stores.append((q, i))
+
+    def row(name, a=0, n=C):
+        return V(name, a, n)
+
+    def col(j):
+        return V("cols", j, 1)
+
+    def five(name, j):
+        return V(name, j, 20, 5)
+
+    def half(name, h, wide=1):
+        return V(name, HC * wide * h, HC * wide)
+
+    def link(out, win, in1, op, k):
+        tt(row(out), row(win), row(in1), op, V("mvo", 20 * k, 20))
+
+    later = []
+
+    def gap(n=1):
+        for _ in range(n):
+            if later:
+                later.pop(0)()
+
+    dma("a", lambda: T.ut[:], lambda: T.u[:], [], [V("ut", 0, 512)])
+    for h in range(2):
+        dma("s", lambda h=h: T.xt[:, 2 * C * h:2 * C * h + 2 * C], lambda h=h: T.x[:, 2 * C * h:2 * C * h + 2 * C], [],
+            [V("xt", 2 * C * h, 2 * C)])
+    dma("s", lambda: T.mvi[:], lambda: T.mv[:], [], [V("mvi", 0, 60)])
+    dma("s", lambda: T.qw[:].bitcast(dt.uint8), lambda: T.wc[:], [], [V("qw", 0, 512)], "w")
+    dma("s", lambda: T.sw[:], lambda: T.ws[:], [], [V("sw", 0, 512)], "w")
+    dma("s", lambda: T.vt[:], lambda: T.v[:], [], [V("vt", 0, 512)])
+
+    iota(V("sm", 0, 8), [[1, 8]], 0, 0, True)
+    iota(V("pi", 0, 2), [[0, 2]], 0, 1, False)
+    iota(row("jr"), [[1, C]], 128, -1, False)
+    iota(row("rr"), [[0, C // 16], [1, 16]], 0, 0, True)
+    iota(V("g8", 0, 512), [[1, 8], [0, 64]], 0, 0, True)
+    iota(row("ii"), [[1, C]], 0, 0, True)
+    iota(V("et", 0, 520), [[0, 520]], 1, 0, True)
+    put("g", "sel", lambda: g.affine_select(T.et[:], T.et[:], [[1, 520]], A.is_equal, 0.0, -3, -4),
+        [V("et", 0, 520)], [V("et", 0, 520)])
+
+    fill(V("zero", 0, 512), 0.0)
+    for a, cnt in ((0, 512), (512, 512), (1024, 256)):
+        af(V("ct", 5 * 4 * C + a, cnt), V("zero", 0, cnt), FN.Copy, grp="ct0")
+    ts(V("uo", 0, 8), V("sm", 0, 8), 16.0, A.mult)
+    ts(V("qi", 0, 2), V("pi", 0, 2), 15, A.bitwise_and)
+    ts(V("gi", 0, 2), V("pi", 0, 2), 4, A.arith_shift_right)
+    quant(V("ql", 0, 128), V("sl", 0, 128), V("zero", 0, 512))
+    ts(V("pa", 0, 2), V("qi", 0, 2), 3, A.bitwise_and)
+    ts(V("pb", 0, 2), V("qi", 0, 2), 2, A.arith_shift_right)
+    cp(col(8), V("qi", 0, 1))
+    ts(row("jj"), row("jr"), 15, A.bitwise_and)
+    ts(col(6), V("pa", 0, 1), 16.0, A.mult)
+    ts(row("mk"), row("jj"), -0.5, A.add, HUGE, A.mult)
+    tt(col(7), col(6), V("pb", 0, 1), A.add)
+    cp(col(0), V("gi", 0, 1))
+    ts(V("po", 0, 4), V("sm", 0, 4), 4.0, A.mult, col(7), A.add)
+    af(row("rs"), row("rr"), FN.Identity, -HUGE, HUGE / 2)
+    quant(V("qu", 0, 128), V("su", 0, 128), V("ut", 0, 512))
+    quant(half("qx", 0), half("sx", 0), half("xt", 0, 4))
+    put("v", "pick", lambda: vec.tensor_copy(T.qp[:].bitcast(dt.uint32), T.qu[:].bitcast(dt.uint32).indirect(T.uo[:])),
+        [V("qu", 0, 128), V("uo", 0, 8)], [V("qp", 0, 128)])
+    put("a", "pick", lambda: act.activation(T.sp[:], T.su[:].indirect(T.uo[:]), FN.Copy),
+        [V("su", 0, 128), V("uo", 0, 8)], [V("sp", 0, 128)])
+
+    def mvi(k):
+        return V("mvi", 20 * k, 20)
+
+    later += [
+        lambda: cp(V("mvo", 0, 60), V("mvi", 0, 60)),
+        lambda: fill(V("bt", 4 * K, 512 - 4 * K), 0.0),
+        lambda: quant(V("qe", 0, 128), V("se", 0, 128), V("et", 3, 512)),
+        lambda: quant(V("qe", 128, 128), V("se", 128, 128), V("et", 2, 512)),
+        lambda: quant(V("qe", 256, 128), V("se", 256, 128), V("et", 1, 512)),
+        lambda: quant(V("qe", 384, 128), V("se", 384, 128), V("et", 0, 512)),
+        lambda: tt(five("h1", 1), mvi(1), mvi(0), A.subtract),
+        lambda: tt(V("d2", 0, 20), mvi(2), mvi(1), A.subtract),
+        lambda: cp(five("h1", 2), mvi(0)),
+        lambda: tt(five("h1", 0), V("d2", 0, 20), five("h1", 1), A.subtract),
+        lambda: fill(five("h0", 0), 0.0),
+        lambda: fill(five("h0", 4), 1.0),
+    ]
+
+    n = len(T.cores)
+    _, relays, dst = road(T, topo, (rank - 1) % n)
+    src_core, in_relays, _ = road(T, topo, rank)
+    arrivals = sum(len(topo.engines(c, core)) for c in (in_relays or [src_core, src_core]))
+    qk, sk = V("qk", 0, 128), V("sk", 0, 128)
+    qp, sp = V("qp", 0, 128), V("sp", 0, 128)
+    qv, sv = V("qv", 0, 128), V("sv", 0, 128)
+    SV, SA, PV, PA, L0 = 0, 1, 2, 3, 4
+
+    def table(h, b):
+        tt(half("d1", h), b, half("mk", h), A.max)
+        if h == 0:
+            gap()
+        scan(half("vv", h), half("rs", h), half("d1", h), A.max, A.min)
+
+    def codes_out(q, h):
+        dma(q, lambda: T.oc[:, 4 * HC * h:4 * HC * h + 4 * HC], lambda: T.qx[:, HC * h:HC * h + HC].bitcast(dt.uint8),
+            [half("qx", h)], [], "o" + q)
+
+    mm(bank(L0, 0, HC), qp, sp, half("qx", 0), half("sx", 0))
+    quant(half("qx", 1), half("sx", 1), half("xt", 1, 4))
+    for e in range(2):
+        af(V("yy", C * e, C), V("xt", e, C, 4), FN.Copy, 32.0)
+
+    for r in range(R):
+        xs = "xt" if r == 0 else "xn"
+        last = r == R - 1
+        mm(bank(SV), qp, sp, row("qx"), row("sx"))
+        mm(bank(SA), qp, sp, row("qx"), row("sx"))
+        if r == 0:
+            ts(V("kt", 0, 512), V("g8", 0, 512), col(0), A.is_equal, 512.0, A.mult)
+        table(0, bank(L0, 0, HC))
+        if r == 0:
+            quant(qk, sk, V("kt", 0, 512))
+
+        def slot(m, a, cnt):
+            return V("ct", 4 * C * (m // 4) + 4 * a + m % 4, cnt, 4)
+
+        def score(m):
+            return V("vv", 16 * m + 15, 1)
+
+        done = []
+
+        def count(tile):
+            quant(V("qc", C * tile, C), V("sc", C * tile, C), V("ct", 4 * C * tile, 4 * C))
+            done.append(tile)
+            for b in (PV, PA):
+                mm(bank(b), qk, sk, V("qc", C * tile, C), V("sc", C * tile, C), len(done) == 1, len(done) == 6, ("pl", r, b))
+
+        def vrow(m):
+            cut = 16 * m + 16
+            ts(slot(m, 0, cut), bank(SV, 0, cut), score(m), A.is_lt, grp=("vr", r, m // 4))
+            if cut < C:
+                ts(slot(m, cut, C - cut), bank(SV, cut, C - cut), score(m), A.is_le, grp=("vr", r, m // 4))
+
+        def arow1(m):
+            af(slot(m, 0, C), bank(SA), FN.Sign, -1.0, score(m))
+
+        def arow2(m):
+            cut = 16 * m + 16
+            af(slot(m, 0, cut), slot(m, 0, cut), FN.Relu, grp=("ar", r, m // 4))
+            af(slot(m, cut, C - cut), slot(m, cut, C - cut), FN.Sign, 1.0, 1.0, grp=("ar", r, m // 4))
+
+        arows = list(range(8, ACT_ROWS)) + list(range(8))
+        arow1(arows[0])
+        for a in range(len(arows)):
+            if a + 1 < len(arows):
+                arow1(arows[a + 1])
+            arow2(arows[a])
+        if r == 0:
+            af(col(1), col(8), FN.Identity, 2048.0, 512.0)
+            af(V("yy", 2 * C, C), V("xt", 2, C, 4), FN.Copy, 32.0)
+            af(V("bias", 0, 8), V("sm", 0, 8), FN.Identity, 512.0, col(1))
+            af(V("yy", 3 * C, C), V("xt", 3, C, 4), FN.Copy, 32.0)
+        table(1, bank(SV, HC, HC))
+        for m in range(ACT_ROWS, 10):
+            vrow(m)
+        tt(slot(20, 0, C), bank(SV), row("vv"), A.is_equal)
+        for m in range(max(ACT_ROWS, 10), 12):
+            vrow(m)
+        count(5)
+        for m in range(16, 20):
+            vrow(m)
+        count(2)
+        count(4)
+        for m in range(12, 14):
+            vrow(m)
+        count(0)
+        for m in range(14, 16):
+            vrow(m)
+        count(3)
+        count(1)
+        if r == 0:
+            ts(row("mm"), row("mk"), -2.0 ** -53, A.mult, -OFF, A.max)
+        gap()
+
+        tt(row("key"), bank(PV), row("ii"), A.add)
+        af(row("s1"), bank(PA), FN.Relu, -512.0, 256.5 * 2 ** 18)
+        scan(row("t1"), row("mm"), bank(PV), A.add, A.min)
+        tt(row("a0"), bank(PV), row("s1"), A.min)
+        gap()
+
+        def sums(m):
+            af(V("junk", C * m, C), row("key"), FN.Relu, -1.0, V("bias", m, 1), acc=V("gs", m, 1), grp=("gs", r))
+
+        sums(0)
+        sums(1)
+        af(row("a1"), row("a0"), FN.Identity, 1.0, 1.0)
+        sums(2)
+        sums(3)
+        sums(4)
+        ts(row("ca"), row("a0"), 2.0, A.add, off=V("mvo", 40, 20))
+        gap()
+        link("cb", "a1", "ca", A.min, 1)
+        gap()
+        link("c1", "a0", "cb", A.min, 0)
+        tt(V("oa", 0, 4), V("gs", 0, 4), V("gs", 1, 4), A.subtract)
+        ts(row("n0"), row("c1"), 3.5, A.is_ge, BB, A.mult)
+        af(row("n1"), row("n0"), FN.Identity, 0.75, AL)
+        tt(V("ob", 0, 4), V("oa", 0, 4), V("bias", 0, 4), A.add)
+        cp(V("oo", 0, 4), V("ob", 0, 4))
+        ts(V("bt", 0, K, 4), V("yy", 0, C), 1.0 / 32, A.mult, off=V("oo", 0, 4))
+        link("ca", "n0", "n1", A.subtract, 0)
+        for e in range(1, 4):
+            af(V("bt", e, K, 4), V("yy", C * e, C), FN.Copy, 1.0 / 32, off=V("oo", 0, 4), grp=("bt", r))
+        af(row("n2"), row("n0"), FN.Identity, 0.5, AL)
+        af(row("s3"), row("c1"), FN.Identity, 1.0, AL - 4.0)
+        quant(V("qb", 128 * r, 128), V("sb", 128 * r, 128), V("bt", 0, 512))
+        link("cb", "n1", "ca", A.max, 1)
+        gap()
+        for part in range(2):
+            if relays is None:
+                fn = lambda part=part, r=r: write(g, T, topo, core, dst, piece(T, "land", part, r), piece(T, "made", part, r), "arr%d" % r)
+            else:
+                fn = lambda part=part, r=r: write(g, T, topo, core, relays[part], piece(T, "mid", part, r), piece(T, "made", part, r), "mid%d" % r)
+            put("g", "send", fn, [V(("qb", "sb")[part], 128 * r, 128)], [])
+        link("c2", "n2", "cb", A.max, 2)
+        gap()
+        af(row("e1"), row("c2"), FN.Identity, 1.0, 1.0)
+        af(row("e2"), row("c2"), FN.Identity, 1.0, 2.0)
+        af(row("s4"), row("c2"), FN.Identity, -4.0 / BB, AL + 6.5)
+        if r == 0:
+            af(col(2), col(8), FN.Identity, -OFF, 15 * OFF)
+            af(col(3), col(2), FN.Identity, -1.0, AL + 10.0)
+            af(col(4), col(2), FN.Identity, 1.0, -512 * 256.5)
+            af(col(5), col(2), FN.Identity, 1.0 / 512, -257.0)
+        t1, sg = V("t1", 15, 20, 16), V("sg", 0, 20)
+        af(sg, t1, FN.Sign, 1.0, col(4))
+        af(five("h1", 3), t1, FN.Relu, 1.0 / 512, col(5), grp=("l0", r))
+        af(five("h0", 3), sg, FN.Relu, -1.0, grp=("l0", r))
+        af(five("h1", 4), sg, FN.Relu, float(C), grp=("l0", r))
+        for e in range(4):
+            af(V("fx", FW * e, C), V("yy", C * e, C), FN.Copy, 1.0 / 32)
+        link("ca", "c2", "s3", A.min, 0)
+        gap()
+        link("cb", "e1", "ca", A.min, 1)
+        gap()
+        link("c3", "e2", "cb", A.min, 2)
+        gap()
+        t3, t4 = V("t3", 15, 20, 16), V("t4", 15, 20, 16)
+        link("ca", "c3", "s4", A.max, 0)
+        scan(row("t3"), row("mm"), row("c3"), A.add, A.min)
+        link("cb", "c3", "ca", A.max, 1)
+        gap()
+        link("c4", "c3", "cb", A.max, 2)
+        gap(len(later))
+        lq, ls = V("ql", K + K * r, 128), V("sl", K + K * r, 128)
+        for e in range(4):
+            mm(bank(L0 + e, 0, 128), V("qe", 128 * e, 128), V("se", 128 * e, 128), lq, ls,
+               ext=[("arr%d" % r, arrivals)] if e == 0 else [])
+        for e in range(5):
+            if e < 4:
+                af(V("dec", K * e, K), bank(L0 + e, K, K), FN.Copy)
+            if e:
+                af(V("fx", FW * (e - 1) + C, K), V("dec", K * (e - 1), K), FN.Copy, off=V("po", 0, 4))
+        for e in range(4):
+            af(V("hh", FW * e + C, K), V("fx", FW * e + C, K), FN.Copy, 2.0)
+        scan(row("t4"), row("mm"), row("c4"), A.add, A.min)
+        ta, tb, kk = V("ta", 0, 20), V("tb", 0, 20), V("kk", 0, 20)
+        ts(ta, t4, col(3), A.is_lt, -2.0 ** 25, A.mult)
+        tt(tb, t4, ta, A.max)
+        tt(V("ki", 0, 20), t3, tb, A.min)
+        ts(kk, V("ki", 0, 20), 3, A.bitwise_and)
+        ts(five("h0", 1), kk, -1.0, A.add, 0.5, A.mult, grp=("kk", r))
+        cp(five("h0", 2), kk, grp=("kk", r))
+        scan(V("ho", 0, 100), V("h0", 0, 100), V("h1", 0, 100), A.mult, A.add)
+        cp(V("to", 0, 20), five("ho", 4))
+        to = V("to", 0, 20)
+        for e in range(4):
+            tt(V("hh", FW * e, C), V("fx", FW * e, FW), V(xs, e, C, 4), A.add, to)
+            if e < 3:
+                af(V("zt", e, C, 4), V("hh", FW * e, FW), FN.Copy, 0.5, off=to)
+        if last:
+            fill(V("tt", 20, 12), 0.0)
+        ts(V("zt", 3, HC, 4), V("hh", FW * 3, FW), 0.5, A.mult, off=V("to", 0, 10))
+        af(V("zt", 3 + 2 * C, HC, 4), V("hh", FW * 3, FW), FN.Copy, 0.5, off=V("to", 10, 10))
+        if last:
+            cp(V("tt", 0, 20), five("ho", 4))
+        for h in range(2):
+            quant(half("qz", h), half("sz", h), half("zt", h, 4))
+            for e in range(4):
+                mm(bank((L0 + e + 4 * h) % 8, 0, HC), V("qw", 128 * e, 128), V("sw", 128 * e, 128), half("qz", h), half("sz", h))
+        if last:
+            put("v", "tr", lambda: vec.transpose(T.tr[:], T.tt[:]), [V("tt", 0, 32)], [V("tr", 0, 32)])
+            for k in range(8):
+                dma("s", lambda k=k: T.ot[k, :], lambda k=k: T.tr[32 * (k // 2):32 * (k // 2) + 20, 16 * (k % 2):16 * (k % 2) + 16],
+                    [V("tr", 0, 32)], [], "ot")
+        if r == 0:
+            quant(qv, sv, V("vt", 0, 512))
+        lhs = (qv, sv) if last else (qp, sp)
+        for h in range(2):
+            for e in range(4):
+                y = V("yy", C * e + HC * h, HC)
+                tt(y, bank((L0 + e + 4 * h) % 8, 0, HC), y, A.add)
+                if (h, e) != (1, 3):
+                    af(V("xn", 2 * C * h + e, HC, 4), y, FN.Copy, 1.0 / 32, grp=("xn", r, h))
+                if (h, e) == (1, 1):
+                    quant(half("qx", 0), half("sx", 0), half("xn", 0, 4))
+                    mm(bank(L0, 0, HC), lhs[0], lhs[1], half("qx", 0), half("sx", 0))
+                    if last:
+                        codes_out("s", 0)
+        ts(V("xn", 2 * C + 3, HC, 4), V("yy", 3 * C + HC, HC), 1.0 / 32, A.mult)
+        quant(half("qx", 1), half("sx", 1), half("xn", 1, 4))
+
+    mm(bank(L0 + 1, 0, HC), qv, sv, half("qx", 1), half("sx", 1))
+    af(half("ys", 0), bank(L0, 0, HC), FN.Copy)
+    cp(half("ys", 1), bank(L0 + 1, 0, HC))
+    dma("s", lambda: T.y[:, 0:HC], lambda: T.ys[:, 0:HC], [half("ys", 0)], [], "os")
+    codes_out("a", 1)
+    for k in range(4):
+        dma("as"[k // 2], lambda k=k: T.osc[4 * k:4 * k + 4, :], lambda k=k: T.sx[32 * k:32 * k + 4, :], [row("sx")], [],
+            "o" + "as"[k // 2])
+    dma("s", lambda: T.y[:, HC:C], lambda: T.ys[:, HC:C], [half("ys", 1)], [], "os")
+    for q in ("s", "a"):
+        put(q, "end", None, [], [], after=[i for qq, i in stores if qq == q])
+    put("g", "end", None, [], [], ext=[("sent", R * sum(len(topo.engines(core, c)) for c in (relays or [dst, dst])))])
+    return ops
+
+
+def rank_program(g, core, T, topo):
+    rank = T.rank_of(core)
+    if rank is None:
+        for r in range(len(T.cores)):
+            src, relays, dst = road(T, topo, r)
+            if relays and core in relays:
+                relay_program(g, core, T, topo, src, dst, relays.index(core))
+        return
+    ops = rank_ops(g, core, T, topo, rank)
+    run(ops, {"g": g, "v": g.vector, "a": g.scalar, "t": g.tensor, "s": g.sync}, T)

@@ -1,13 +1,21 @@
+import math
 from concourse.mybir import dt, AluOpType, ActivationFunctionType
 
 C, K, R = 320, 64, 3
 HC = C // 2
 FW = C + K
-BB = 524288.0
-AL = -0.375 * BB
-OFF = 262144.0
+CW = C + 16
+FRAC = 4096.0
+OFF1 = 512.0
+OFF2 = 16.0
 HUGE = 2.0 ** 80
-ACT_ROWS = 9
+CUT1, CUT3 = 160, 96
+TILES = ((0, 320, (9, 0)), (320, 128, (1, 2)), (448, 128, (3, 4)), (576, 192, (5, 6)), (768, 256, (7, 8)))
+CTW = 1024
+ACT_EARLY = ((4, 0), (3, 0), (4, 1), (3, 1))
+ACT_LATE = ((9, 0), (8, 0), (9, 1), (8, 1), (7, 0), (7, 1))
+VEC_ROWS = ((1, 0), (1, 1), (2, 0), (2, 1), (5, 0), (5, 1), (6, 0), (6, 1))
+RS = 96
 
 F32, BF, I32, U16, MX, U8 = "float32", "bfloat16", "int32", "uint16", "float8_e4m3fn_x4", "uint8"
 
@@ -18,29 +26,37 @@ def _sb(n, d):
 
 SCRATCH = {
     "xt": _sb(4 * C, BF), "xn": _sb(4 * C, BF), "ut": _sb(512, BF), "vt": _sb(512, BF),
-    "qu": _sb(128, MX), "su": _sb(128, U8), "qp": _sb(128, MX), "sp": _sb(128, U8),
+    "qu": _sb(128, MX), "su": _sb(128, U8), "qp": _sb(256, MX), "sp": _sb(256, U8),
+    "vv": _sb(2 * C, F32), "d1": _sb(2 * C, F32), "rb": _sb(20 * RS, F32), "cm": _sb(2 * 176, BF),
+    "rd": _sb(20, F32), "re": _sb(20, F32), "cs": _sb(20, F32), "uf": _sb(16, F32), "cb": _sb(20, BF),
     "qv": _sb(128, MX), "sv": _sb(128, U8), "qx": _sb(C, MX), "sx": _sb(C, U8),
     "qw": _sb(512, MX), "sw": _sb(512, U8), "qz": _sb(C, MX), "sz": _sb(C, U8),
     "qk": _sb(128, MX), "sk": _sb(128, U8), "qe": _sb(512, MX), "se": _sb(512, U8),
-    "qc": _sb(6 * C, MX), "sc": _sb(6 * C, U8),
+    "qc": _sb(CTW, MX), "sc": _sb(CTW, U8),
     "qb": _sb(128 * R, MX), "sb": _sb(128 * R, U8),
     "qr": _sb(K * R, MX), "sr": _sb(K * R, U8),
     "ql": _sb(128 + K * R, MX), "sl": _sb(128 + K * R, U8),
-    "mvi": _sb(60, I32), "mvo": _sb(60, U16), "d2": _sb(20, F32),
-    "yy": _sb(4 * C, BF), "fx": _sb(4 * FW, BF), "hh": _sb(4 * FW, F32), "zt": _sb(4 * C, BF),
-    "bt": _sb(512, BF), "zero": _sb(512, BF), "ct": _sb(6 * 4 * C, BF), "et": _sb(520, BF),
-    "kt": _sb(512, BF), "g8": _sb(512, BF), "dec": _sb(4 * K, F32), "ys": _sb(C, F32),
-    "pi": _sb(2, I32), "qi": _sb(2, I32), "gi": _sb(2, I32), "pa": _sb(2, I32), "pb": _sb(2, I32),
-    "cols": _sb(16, F32), "sm": _sb(8, F32), "uo": _sb(8, U16), "po": _sb(4, U16), "bias": _sb(8, F32),
+    "mvi": _sb(60, I32), "mvo": _sb(60, U16), "m2o": _sb(20, U16), "d2": _sb(20, F32),
+    "yy": _sb(4 * FW, BF), "fx": _sb(4 * FW, BF), "hh": _sb(4 * FW, F32), "zt": _sb(4 * C, BF),
+    "bt": _sb(512, BF), "zero": _sb(512, BF), "ct": _sb(4 * CTW, BF), "et": _sb(520, BF),
+    "kt": _sb(512, BF), "g8": _sb(512, BF), "ys": _sb(C, F32),
+    "pi": _sb(2, I32), "qi": _sb(2, I32), "gi": _sb(2, I32), "ri": _sb(2, I32),
+    "cols": _sb(16, F32), "sm": _sb(8, F32), "uo": _sb(16, U16), "bias": _sb(8, F32),
     "tt": _sb(32, F32), "tr": _sb(32, F32), "to": _sb(20, U16),
-    "jr": _sb(C, I32), "jj": _sb(C, I32), "junk": _sb(5 * C, F32),
+    "junk": _sb(5 * C, F32),
     "gs": _sb(8, F32), "oa": _sb(4, F32), "ob": _sb(4, F32), "oo": _sb(4, U16),
-    "ta": _sb(20, F32), "tb": _sb(20, F32), "ki": _sb(20, I32), "kk": _sb(20, I32), "sg": _sb(20, F32),
-    "h0": _sb(100, F32), "h1": _sb(100, F32), "ho": _sb(100, F32),
+    "f1": _sb(20, F32), "m2": _sb(20, F32), "ki": _sb(20, I32), "k1": _sb(20, I32), "al": _sb(20, F32),
+    "am": _sb(20, F32), "kb": _sb(20, F32), "zi": _sb(40, I32), "kk": _sb(40, I32), "sg": _sb(20, F32),
+    "h0": _sb(120, F32), "h1": _sb(120, F32), "ho": _sb(120, F32),
+    "g0": _sb(140, F32), "g1": _sb(140, F32), "go": _sb(140, F32), "hb": _sb(20, BF),
     "ps": ("psum", [128, 512 * 8], F32),
 }
-for _n in ("rr ii mk rs mm d1 vv key a0 a1 s1 ca cb c1 c2 c3 c4 n0 n1 n2 e1 e2 s3 s4 t1 t3 t4").split():
+for _n in ("mm hm hi hd ov key a0 a1 s1 xa xb c1 t1 u1").split():
     SCRATCH[_n] = _sb(C, F32)
+for _n in ("rr", "r16", "mk", "rs"):
+    SCRATCH[_n] = _sb(HC, BF)
+for _n in ("n0 c2 e1 c3 c4 ya yb yc m2b u2 u3 u4 u5").split():
+    SCRATCH[_n] = _sb(CW, BF)
 POOL = ["p%d" % i for i in range(110)]
 SEMAPHORES = POOL + ["arr%d" % r for r in range(R)] + ["mid%d" % r for r in range(R)] + ["sent"]
 
@@ -63,7 +79,7 @@ def _meet(u, v):
         return u[1] // 512 == v[1] // 512
     if u[1] + (u[2] - 1) * u[3] < v[1] or v[1] + (v[2] - 1) * v[3] < u[1]:
         return False
-    return u[3] != v[3] or (u[1] - v[1]) % u[3] == 0
+    return (u[1] - v[1]) % max(math.gcd(u[3] * (u[2] > 1), v[3] * (v[2] > 1)), 1) == 0
 
 
 def road(T, topo, r):
@@ -193,8 +209,8 @@ def rank_ops(g, core, T, topo, rank):
     def cp(out, in0, off=None, grp=None):
         put("v", "cp " + out[0], lambda: vec.tensor_copy(ap(out), src(in0, off)), views(in0, off), [out], grp)
 
-    def scan(out, d0, d1, op0, op1):
-        put("v", "scan " + out[0], lambda: vec.tensor_tensor_scan(ap(out), ap(d0), ap(d1), 0.0, op0, op1), [d0, d1], [out])
+    def scan(out, d0, d1, op0, op1, first=0.0, grp=None):
+        put("v", "scan " + out[0], lambda: vec.tensor_tensor_scan(ap(out), ap(d0), ap(d1), first, op0, op1), [d0, d1], [out], grp)
 
     def fill(out, c):
         put("v", "fill " + out[0], lambda: vec.memset(ap(out), c), [], [out])
@@ -236,14 +252,28 @@ def rank_ops(g, core, T, topo, rank):
     def col(j):
         return V("cols", j, 1)
 
-    def five(name, j):
-        return V(name, j, 20, 5)
+    def tab(name, a=0):
+        return V(name, a, 20)
+
+    def ends(name):
+        return V(name, 15, 20, 16)
+
+    def three(name, j, a=0, n=40):
+        return V(name, 3 * a + j, n, 3)
+
+    def six(name, j):
+        return V(name, j + 1, 20, 7)
 
     def half(name, h, wide=1):
         return V(name, HC * wide * h, HC * wide)
 
-    def link(out, win, in1, op, k):
-        tt(row(out), row(win), row(in1), op, V("mvo", 20 * k, 20))
+    def plane(name, e, a=0, n=C):
+        return V(name, FW * e + a, n)
+
+    m0, m1, m2, m2x = V("mvo", 0, 20), V("mvo", 20, 20), V("mvo", 40, 20), V("m2o", 0, 20)
+
+    def link(out, win, in1, op, off):
+        tt(row(out), row(win, 0, CW if off == m2x else C), row(in1), op, off)
 
     later = []
 
@@ -261,56 +291,71 @@ def rank_ops(g, core, T, topo, rank):
     dma("s", lambda: T.sw[:], lambda: T.ws[:], [], [V("sw", 0, 512)], "w")
     dma("s", lambda: T.vt[:], lambda: T.v[:], [], [V("vt", 0, 512)])
 
-    iota(V("sm", 0, 8), [[1, 8]], 0, 0, True)
+    iota(V("uf", 0, 16), [[16, 2], [32, 4], [0, 2]], 0, 0, True)
     iota(V("pi", 0, 2), [[0, 2]], 0, 1, False)
-    iota(row("jr"), [[1, C]], 128, -1, False)
-    iota(row("rr"), [[0, C // 16], [1, 16]], 0, 0, True)
-    iota(V("g8", 0, 512), [[1, 8], [0, 64]], 0, 0, True)
-    iota(row("ii"), [[1, C]], 0, 0, True)
-    iota(V("et", 0, 520), [[0, 520]], 1, 0, True)
+    fill(V("et", 0, 520), 1.0)
     put("g", "sel", lambda: g.affine_select(T.et[:], T.et[:], [[1, 520]], A.is_equal, 0.0, -3, -4),
         [V("et", 0, 520)], [V("et", 0, 520)])
+    iota(V("rr", 0, HC), [[0, HC // 32], [1, 32]], 0, 0, True)
+    iota(V("r16", 0, HC), [[0, HC // 16], [1, 16]], 0, 0, True)
+    iota(tab("cs"), [[32, 10], [0, 2]], 32, 0, True)
+    iota(V("sm", 0, 8), [[1, 8]], 0, 0, True)
+    iota(V("g8", 0, 512), [[1, 8], [0, 32], [-1, 2]], 0, 0, True)
+
+    def afill(out, c, grp=None):
+        af(out, V("zero", 0, out[2]), FN.Identity, 1.0, c, grp=grp)
 
     fill(V("zero", 0, 512), 0.0)
-    for a, cnt in ((0, 512), (512, 512), (1024, 256)):
-        af(V("ct", 5 * 4 * C + a, cnt), V("zero", 0, cnt), FN.Copy, grp="ct0")
-    ts(V("uo", 0, 8), V("sm", 0, 8), 16.0, A.mult)
+    for a, cnt, blocks in TILES:
+        low = 32 * min(b for b in blocks if b)
+        afill(V("ct", 4 * (a + low), 4 * (cnt - low)), 0.0, "ct0")
+    afill(row("hi"), 0.0)
+    afill(row("hm"), 1.0)
+    for v, c in ((V("n0", C, 16), 7.0), (V("hm", 0, 20, 16), 0.0), (V("e1", C, 16), -1.0), (V("c3", C, 16), 15.0)):
+        afill(v, c)
+    cp(V("uo", 0, 16), V("uf", 0, 16))
     ts(V("qi", 0, 2), V("pi", 0, 2), 15, A.bitwise_and)
-    ts(V("gi", 0, 2), V("pi", 0, 2), 4, A.arith_shift_right)
+    ts(V("gi", 0, 2), V("pi", 0, 2), 5, A.arith_shift_right)
+    ts(V("ri", 0, 2), V("pi", 0, 2), 31, A.bitwise_and)
+    fill(V("rs", 0, HC), HUGE)
     quant(V("ql", 0, 128), V("sl", 0, 128), V("zero", 0, 512))
-    ts(V("pa", 0, 2), V("qi", 0, 2), 3, A.bitwise_and)
-    ts(V("pb", 0, 2), V("qi", 0, 2), 2, A.arith_shift_right)
     cp(col(8), V("qi", 0, 1))
-    ts(row("jj"), row("jr"), 15, A.bitwise_and)
-    ts(col(6), V("pa", 0, 1), 16.0, A.mult)
-    ts(row("mk"), row("jj"), -0.5, A.add, HUGE, A.mult)
-    tt(col(7), col(6), V("pb", 0, 1), A.add)
-    cp(col(0), V("gi", 0, 1))
-    ts(V("po", 0, 4), V("sm", 0, 4), 4.0, A.mult, col(7), A.add)
-    af(row("rs"), row("rr"), FN.Identity, -HUGE, HUGE / 2)
+    cp(col(7), V("ri", 0, 1))
+    ts(col(0), V("gi", 0, 1), 2.0, A.mult)
+    ts(col(6), V("ri", 0, 1), 1 / FRAC - 1, A.mult, -32 / FRAC, A.add)
+    fill(V("rs", 0, HC // 32, 32), -HUGE)
+    fill(V("cm", 15, 2, 176), -128.0)
+    fill(V("rb", RS - 1, 2, RS), 0.0)
+    fill(V("bt", 4 * K, 512 - 4 * K), 0.0)
+    for e in range(4):
+        quant(V("qe", 128 * e, 128), V("se", 128 * e, 128), V("et", 3 - e, 512))
+    ts(V("mk", 0, HC), V("rr", 0, HC), col(7), A.not_equal, -HUGE, A.mult)
     quant(V("qu", 0, 128), V("su", 0, 128), V("ut", 0, 512))
     quant(half("qx", 0), half("sx", 0), half("xt", 0, 4))
-    put("v", "pick", lambda: vec.tensor_copy(T.qp[:].bitcast(dt.uint32), T.qu[:].bitcast(dt.uint32).indirect(T.uo[:])),
-        [V("qu", 0, 128), V("uo", 0, 8)], [V("qp", 0, 128)])
-    put("a", "pick", lambda: act.activation(T.sp[:], T.su[:].indirect(T.uo[:]), FN.Copy),
-        [V("su", 0, 128), V("uo", 0, 8)], [V("sp", 0, 128)])
+    for p in range(2):
+        put("v", "pick", lambda p=p: vec.tensor_copy(T.qp[:, 128 * p:128 * p + 128].bitcast(dt.uint32),
+                                                     T.qu[:].bitcast(dt.uint32).indirect(T.uo[:, 8 * p:8 * p + 8])),
+            [V("qu", 0, 128), V("uo", 8 * p, 8)], [V("qp", 128 * p, 128)])
+        put("a", "pick", lambda p=p: act.activation(T.sp[:, 128 * p:128 * p + 128], T.su[:].indirect(T.uo[:, 8 * p:8 * p + 8]), FN.Copy),
+            [V("su", 0, 128), V("uo", 8 * p, 8)], [V("sp", 128 * p, 128)])
+
+    af(col(1), col(8), FN.Identity, 4.0, 1.0)
+    af(col(3), col(8), FN.Identity, OFF1, 0.5 - 15 * OFF1)
+    af(col(4), col(8), FN.Identity, -OFF1, 15 * OFF1 - 256.5)
+    af(col(5), col(8), FN.Identity, -OFF1, 15 * OFF1 + 128 - 257.0)
+    af(col(10), col(8), FN.Identity, OFF2, 4 - 15 * OFF2)
+    af(col(11), col(8), FN.Identity, OFF2, 9 - 15 * OFF2)
+    af(V("bias", 0, 8), V("sm", 0, 8), FN.Identity, 1.0, col(1))
 
     def mvi(k):
         return V("mvi", 20 * k, 20)
 
     later += [
         lambda: cp(V("mvo", 0, 60), V("mvi", 0, 60)),
-        lambda: fill(V("bt", 4 * K, 512 - 4 * K), 0.0),
-        lambda: quant(V("qe", 0, 128), V("se", 0, 128), V("et", 3, 512)),
-        lambda: quant(V("qe", 128, 128), V("se", 128, 128), V("et", 2, 512)),
-        lambda: quant(V("qe", 256, 128), V("se", 256, 128), V("et", 1, 512)),
-        lambda: quant(V("qe", 384, 128), V("se", 384, 128), V("et", 0, 512)),
-        lambda: tt(five("h1", 1), mvi(1), mvi(0), A.subtract),
-        lambda: tt(V("d2", 0, 20), mvi(2), mvi(1), A.subtract),
-        lambda: cp(five("h1", 2), mvi(0)),
-        lambda: tt(five("h1", 0), V("d2", 0, 20), five("h1", 1), A.subtract),
-        lambda: fill(five("h0", 0), 0.0),
-        lambda: fill(five("h0", 4), 1.0),
+        lambda: tt(three("h1", 1, 0, 20), mvi(1), mvi(0), A.subtract),
+        lambda: tt(tab("d2"), mvi(2), mvi(1), A.subtract),
+        lambda: cp(three("h1", 2, 0, 20), mvi(0)),
+        lambda: tt(three("h1", 0, 0, 20), tab("d2"), three("h1", 1, 0, 20), A.subtract),
     ]
 
     n = len(T.cores)
@@ -318,199 +363,237 @@ def rank_ops(g, core, T, topo, rank):
     src_core, in_relays, _ = road(T, topo, rank)
     arrivals = sum(len(topo.engines(c, core)) for c in (in_relays or [src_core, src_core]))
     qk, sk = V("qk", 0, 128), V("sk", 0, 128)
-    qp, sp = V("qp", 0, 128), V("sp", 0, 128)
     qv, sv = V("qv", 0, 128), V("sv", 0, 128)
-    SV, SA, PV, PA, L0 = 0, 1, 2, 3, 4
+    SV, SA, L0, PV = 0, 2, 4, 7
 
-    def table(h, b):
-        tt(half("d1", h), b, half("mk", h), A.max)
-        if h == 0:
-            gap()
-        scan(half("vv", h), half("rs", h), half("d1", h), A.max, A.min)
+    def scores(b, n):
+        for p in range(2):
+            mm(bank(b + p, 0, n), V("qp", 128 * p, 128), V("sp", 128 * p, 128), V("qx", 0, n), V("sx", 0, n))
+
+    def mask(h, b, p):
+        tt(V("d1", C * p + HC * h, HC), bank(b + p, HC * h, HC), V("mk", 0, HC), A.add)
+
+    def hold(h, p):
+        scan(V("vv", C * p + HC * h, HC), V("rs", 0, HC), V("d1", C * p + HC * h, HC), A.min, A.max)
+
+    def lane(m, p, a=0, step=1, n=None):
+        first, cnt, blocks = [t for t in TILES if m in t[2]][0]
+        return V("ct", 4 * (first + a) + 2 * blocks.index(m) + p, (n or 32 * m or C) // step, 4 * step)
+
+    def score(m, p):
+        return V("vv", C * p + 32 * m + 31, 1)
+
+    def total(m, p, n=1):
+        return V("rb", RS * (2 * m + p + 1) - n, n)
+
+    def pack(t):
+        a, cnt, blocks = TILES[t]
+        quant(V("qc", a, cnt), V("sc", a, cnt), V("ct", 4 * a, 4 * cnt))
+
+    def count(t, r):
+        a, cnt, blocks = TILES[t]
+        mm(bank(PV, 0, cnt), qk, sk, V("qc", a, cnt), V("sc", a, cnt), t == 0, t == len(TILES) - 1, ("pl", r))
+
+    def arows(rows, b):
+        for k in range(len(rows) + 1):
+            if k < len(rows):
+                m, p = rows[k]
+                af(lane(m, p), bank(b + p, 0, 32 * m), FN.Sign, -1.0, score(m, p))
+            if k:
+                m, p = rows[k - 1]
+                af(lane(m, p), lane(m, p), FN.Relu, acc=total(m, p))
+
+    def vrows(rows, b):
+        for m, p in rows:
+            ts(lane(m, p), bank(b + p, 0, 32 * m), score(m, p), A.is_lt)
+
+    def vsums(rows, r):
+        for m, p in rows:
+            scan(total(m, p, 16 * m), lane(m, p, 0, 2), lane(m, p, 1, 2), A.add, A.add, grp=("vs", r))
+
+    def inner(h, b, p):
+        tt(lane(0, p, HC * h, 1, HC), bank(b + p, HC * h, HC), V("vv", C * p + HC * h, HC), A.is_le)
 
     def codes_out(q, h):
         dma(q, lambda: T.oc[:, 4 * HC * h:4 * HC * h + 4 * HC], lambda: T.qx[:, HC * h:HC * h + HC].bitcast(dt.uint8),
             [half("qx", h)], [], "o" + q)
 
-    mm(bank(L0, 0, HC), qp, sp, half("qx", 0), half("sx", 0))
+    scores(L0, HC)
+    scores(L0 + 2, HC)
     quant(half("qx", 1), half("sx", 1), half("xt", 1, 4))
-    for e in range(2):
-        af(V("yy", C * e, C), V("xt", e, C, 4), FN.Copy, 32.0)
+    for p in range(2):
+        mask(0, L0, p)
+    for p in range(2):
+        hold(0, p)
 
     for r in range(R):
-        xs = "xt" if r == 0 else "xn"
         last = r == R - 1
-        mm(bank(SV), qp, sp, row("qx"), row("sx"))
-        mm(bank(SA), qp, sp, row("qx"), row("sx"))
+        for p in range(2):
+            for b in (SV, SA):
+                mm(bank(b + p), V("qp", 128 * p, 128), V("sp", 128 * p, 128), row("qx"), row("sx"))
+        arows(ACT_EARLY, L0 + 2)
+        inner(0, L0, 0)
+        mask(1, SV, 0)
+        inner(0, L0, 1)
+        hold(1, 0)
+        mask(1, SV, 1)
+        inner(1, SV, 0)
+        hold(1, 1)
+        arows(ACT_LATE, SA)
         if r == 0:
-            ts(V("kt", 0, 512), V("g8", 0, 512), col(0), A.is_equal, 512.0, A.mult)
-        table(0, bank(L0, 0, HC))
+            ts(V("r16", 0, HC), V("r16", 0, HC), col(8), A.is_equal)
+            for h in range(2):
+                af(half("mm", h), V("r16", 0, HC), FN.Identity, 2.0 ** 26, -OFF1)
+        for e in range(4):
+            af(plane("fx", e), V("xn" if r else "xt", e, C, 4), FN.Copy)
+        inner(1, SV, 1)
+        if r == 0:
+            ts(V("kt", 0, 512), V("g8", 0, 512), col(0), A.is_equal)
+        vrows(VEC_ROWS[:4], SV)
         if r == 0:
             quant(qk, sk, V("kt", 0, 512))
-
-        def slot(m, a, cnt):
-            return V("ct", 4 * C * (m // 4) + 4 * a + m % 4, cnt, 4)
-
-        def score(m):
-            return V("vv", 16 * m + 15, 1)
-
-        done = []
-
-        def count(tile):
-            quant(V("qc", C * tile, C), V("sc", C * tile, C), V("ct", 4 * C * tile, 4 * C))
-            done.append(tile)
-            for b in (PV, PA):
-                mm(bank(b), qk, sk, V("qc", C * tile, C), V("sc", C * tile, C), len(done) == 1, len(done) == 6, ("pl", r, b))
-
-        def vrow(m):
-            cut = 16 * m + 16
-            ts(slot(m, 0, cut), bank(SV, 0, cut), score(m), A.is_lt, grp=("vr", r, m // 4))
-            if cut < C:
-                ts(slot(m, cut, C - cut), bank(SV, cut, C - cut), score(m), A.is_le, grp=("vr", r, m // 4))
-
-        def arow1(m):
-            af(slot(m, 0, C), bank(SA), FN.Sign, -1.0, score(m))
-
-        def arow2(m):
-            cut = 16 * m + 16
-            af(slot(m, 0, cut), slot(m, 0, cut), FN.Relu, grp=("ar", r, m // 4))
-            af(slot(m, cut, C - cut), slot(m, cut, C - cut), FN.Sign, 1.0, 1.0, grp=("ar", r, m // 4))
-
-        arows = list(range(8, ACT_ROWS)) + list(range(8))
-        arow1(arows[0])
-        for a in range(len(arows)):
-            if a + 1 < len(arows):
-                arow1(arows[a + 1])
-            arow2(arows[a])
+        for p in range(2):
+            scan(V("cm", 176 * p + 16, HC), lane(0, p, 0, 2), lane(0, p, 1, 2), A.add, A.add, -128.0)
+        pack(1)
+        vrows(VEC_ROWS[4:], SV)
+        pack(2)
+        pack(0)
+        for t in range(3):
+            count(t, r)
         if r == 0:
-            af(col(1), col(8), FN.Identity, 2048.0, 512.0)
-            af(V("yy", 2 * C, C), V("xt", 2, C, 4), FN.Copy, 32.0)
-            af(V("bias", 0, 8), V("sm", 0, 8), FN.Identity, 512.0, col(1))
-            af(V("yy", 3 * C, C), V("xt", 3, C, 4), FN.Copy, 32.0)
-        table(1, bank(SV, HC, HC))
-        for m in range(ACT_ROWS, 10):
-            vrow(m)
-        tt(slot(20, 0, C), bank(SV), row("vv"), A.is_equal)
-        for m in range(max(ACT_ROWS, 10), 12):
-            vrow(m)
-        count(5)
-        for m in range(16, 20):
-            vrow(m)
-        count(2)
-        count(4)
-        for m in range(12, 14):
-            vrow(m)
-        count(0)
-        for m in range(14, 16):
-            vrow(m)
-        count(3)
-        count(1)
-        if r == 0:
-            ts(row("mm"), row("mk"), -2.0 ** -53, A.mult, -OFF, A.max)
+            ts(tab("cs"), tab("cs"), 1 + 1 / FRAC, A.mult, col(6), A.add)
+        for p in range(2):
+            tt(V("rd", p, 10, 2), V("cm", 176 * p + 15, 10, 16), V("cm", 176 * p + 31, 10, 16), A.subtract, grp=("rd", r))
+        vsums(VEC_ROWS[:4], r)
+        tt(tab("re"), tab("rd"), tab("cs"), A.add)
+        vsums(VEC_ROWS[4:], r)
+        pack(3)
+        count(3, r)
+        tt(V("hi", 0, 20, 16), tab("re"), V("rb", RS - 1, 20, RS), A.subtract)
+        pack(4)
+        count(4, r)
+        scan(row("hd"), row("hm"), row("hi"), A.mult, A.add)
         gap()
-
-        tt(row("key"), bank(PV), row("ii"), A.add)
-        af(row("s1"), bank(PA), FN.Relu, -512.0, 256.5 * 2 ** 18)
-        scan(row("t1"), row("mm"), bank(PV), A.add, A.min)
-        tt(row("a0"), bank(PV), row("s1"), A.min)
-        gap()
+        put("v", "tr", lambda: vec.transpose(T.ov[:], T.hd[:]), [row("hd")], [row("ov")])
 
         def sums(m):
             af(V("junk", C * m, C), row("key"), FN.Relu, -1.0, V("bias", m, 1), acc=V("gs", m, 1), grp=("gs", r))
 
+        gap()
+        tt(row("key"), bank(PV), row("ov"), A.add)
+        gap()
+        af(row("s1"), row("key"), FN.Relu, -1024.0, 1024 * 256.5)
+        scan(row("t1"), row("mm"), row("key"), A.add, A.min)
+        tt(row("a0"), row("key"), row("s1"), A.min)
         sums(0)
         sums(1)
-        af(row("a1"), row("a0"), FN.Identity, 1.0, 1.0)
-        sums(2)
-        sums(3)
-        sums(4)
-        ts(row("ca"), row("a0"), 2.0, A.add, off=V("mvo", 40, 20))
+        af(row("xa", CUT1, C - CUT1), row("a0"), FN.Identity, 1.0, -0.25, off=V("mvo", CUT1 // 16, 20 - CUT1 // 16))
+        af(row("a1"), row("a0"), FN.Identity, 1.0, 0.25)
+        for m in range(2, 5):
+            sums(m)
         gap()
-        link("cb", "a1", "ca", A.min, 1)
+        ts(row("xa", 0, CUT1), row("a0"), -0.25, A.add, off=V("mvo", 0, CUT1 // 16))
+        gap(2)
+        link("xb", "a0", "xa", A.min, m1)
         gap()
-        link("c1", "a0", "cb", A.min, 0)
+        link("c1", "a1", "xb", A.min, m2)
+        gap()
+        ts(row("n0"), row("c1"), 0.5, A.is_ge, 7.0, A.mult)
+        af(row("ya"), row("n0"), FN.Identity, 8.0 / 7, 1.0, off=m0)
         tt(V("oa", 0, 4), V("gs", 0, 4), V("gs", 1, 4), A.subtract)
-        ts(row("n0"), row("c1"), 3.5, A.is_ge, BB, A.mult)
-        af(row("n1"), row("n0"), FN.Identity, 0.75, AL)
+        scan(row("u1"), row("mm"), row("c1"), A.add, A.min)
         tt(V("ob", 0, 4), V("oa", 0, 4), V("bias", 0, 4), A.add)
-        cp(V("oo", 0, 4), V("ob", 0, 4))
-        ts(V("bt", 0, K, 4), V("yy", 0, C), 1.0 / 32, A.mult, off=V("oo", 0, 4))
-        link("ca", "n0", "n1", A.subtract, 0)
+        ts(tab("f1"), ends("u1"), col(3), A.is_lt, float(C), A.mult)
+        ts(V("oo", 0, 4), V("ob", 0, 4), FRAC, A.mult)
+        tt(tab("m2"), tab("f1"), mvi(2), A.max)
         for e in range(1, 4):
-            af(V("bt", e, K, 4), V("yy", C * e, C), FN.Copy, 1.0 / 32, off=V("oo", 0, 4), grp=("bt", r))
-        af(row("n2"), row("n0"), FN.Identity, 0.5, AL)
-        af(row("s3"), row("c1"), FN.Identity, 1.0, AL - 4.0)
+            af(V("bt", e, K, 4), plane("fx", e), FN.Copy, off=V("oo", 0, 4), grp=("bt", r))
+        cp(V("bt", 0, K, 4), plane("fx", 0), off=V("oo", 0, 4))
+        link("yb", "n0", "ya", A.add, m1)
         quant(V("qb", 128 * r, 128), V("sb", 128 * r, 128), V("bt", 0, 512))
-        link("cb", "n1", "ca", A.max, 1)
-        gap()
+        cp(m2x, tab("m2"))
         for part in range(2):
             if relays is None:
                 fn = lambda part=part, r=r: write(g, T, topo, core, dst, piece(T, "land", part, r), piece(T, "made", part, r), "arr%d" % r)
             else:
                 fn = lambda part=part, r=r: write(g, T, topo, core, relays[part], piece(T, "mid", part, r), piece(T, "made", part, r), "mid%d" % r)
             put("g", "send", fn, [V(("qb", "sb")[part], 128 * r, 128)], [])
-        link("c2", "n2", "cb", A.max, 2)
-        gap()
-        af(row("e1"), row("c2"), FN.Identity, 1.0, 1.0)
-        af(row("e2"), row("c2"), FN.Identity, 1.0, 2.0)
-        af(row("s4"), row("c2"), FN.Identity, -4.0 / BB, AL + 6.5)
+        af(tab("cb"), ends("t1"), FN.Identity, 1.0, col(5))
+        af(tab("sg"), ends("t1"), FN.Sign, 1.0, col(4))
+        af(six("g1", 2), tab("cb"), FN.Relu, 1.0, -128.0)
+        af(six("g0", 2), tab("sg"), FN.Relu, -1.0, grp=("l0", r))
+        af(tab("hb"), six("g1", 2), FN.Identity, 0.25, 159.625)
+        af(six("g1", 3), tab("sg"), FN.Relu, float(C), grp=("l0", r))
+        af(six("g1", 4), six("g1", 2), FN.Copy, 15.0, grp=("l0", r))
+        af(six("g1", 5), tab("hb"), FN.Identity, -63.0, 63.0 * 160, grp=("l0", r))
         if r == 0:
-            af(col(2), col(8), FN.Identity, -OFF, 15 * OFF)
-            af(col(3), col(2), FN.Identity, -1.0, AL + 10.0)
-            af(col(4), col(2), FN.Identity, 1.0, -512 * 256.5)
-            af(col(5), col(2), FN.Identity, 1.0 / 512, -257.0)
-        t1, sg = V("t1", 15, 20, 16), V("sg", 0, 20)
-        af(sg, t1, FN.Sign, 1.0, col(4))
-        af(five("h1", 3), t1, FN.Relu, 1.0 / 512, col(5), grp=("l0", r))
-        af(five("h0", 3), sg, FN.Relu, -1.0, grp=("l0", r))
-        af(five("h1", 4), sg, FN.Relu, float(C), grp=("l0", r))
-        for e in range(4):
-            af(V("fx", FW * e, C), V("yy", C * e, C), FN.Copy, 1.0 / 32)
-        link("ca", "c2", "s3", A.min, 0)
+            for h in range(2):
+                af(half("m2b", h), V("r16", 0, HC), FN.Identity, 2.0 ** 26, -OFF2)
+        link("c2", "n0", "yb", A.max, m2x)
+        af(row("ya", CUT3, C - CUT3), row("c2"), FN.Identity, 1.0, -1.0, off=V("mvo", CUT3 // 16, 20 - CUT3 // 16))
+        af(row("e1"), row("c2"), FN.Identity, 1.0, 1.0)
+        ts(tab("ki"), ends("u1"), 4.0, A.mult, 1.0, A.add)
+        ts(row("ya", 0, CUT3), row("c2"), -1.0, A.add, off=V("mvo", 0, CUT3 // 16))
+        scan(row("u2"), row("m2b"), row("c2"), A.add, A.min)
+        ts(tab("k1"), tab("ki"), 3, A.bitwise_and)
         gap()
-        link("cb", "e1", "ca", A.min, 1)
-        gap()
-        link("c3", "e2", "cb", A.min, 2)
-        gap()
-        t3, t4 = V("t3", 15, 20, 16), V("t4", 15, 20, 16)
-        link("ca", "c3", "s4", A.max, 0)
-        scan(row("t3"), row("mm"), row("c3"), A.add, A.min)
-        link("cb", "c3", "ca", A.max, 1)
-        gap()
-        link("c4", "c3", "cb", A.max, 2)
-        gap(len(later))
+        tt(tab("al"), tab("k1"), tab("f1"), A.subtract)
+        gap(2)
+        af(tab("kb"), ends("u2"), FN.Relu, -1.0, col(11))
+        af(tab("am"), tab("al"), FN.Identity, 1.0, col(10))
+        if r == 0:
+            afill(three("h0", 0), 0.0)
+            af(V("h1", 60, 60), V("h1", 0, 60), FN.Copy)
+            for j, c in ((-1, 0.0), (3, 1.0), (4, 1.0), (5, 1.0)):
+                afill(six("g0", j), c)
+            afill(six("g1", 0), 0.0)
+            af(plane("yy", 0), V("xt", 0, C, 4), FN.Copy, 32.0)
+        link("yb", "c2", "ya", A.min, m1)
+        cp(tab("zi", 20), tab("kb"))
+        link("c3", "e1", "yb", A.min, m2x)
+        af(row("ya"), row("c3"), FN.Copy, off=m0)
+        af(row("yc"), row("c3"), FN.Copy, off=m1)
+
+        scan(row("u3"), row("m2b"), row("c3"), A.add, A.min)
+        tt(tab("zi"), ends("u3"), tab("am"), A.min)
+        kk = V("kk", 0, 40)
+        ts(kk, V("zi", 0, 40), 3, A.bitwise_and)
+        ts(three("h0", 1), kk, -1.0, A.add, 0.5, A.mult, grp=("kk", r))
+        cp(three("h0", 2), kk, grp=("kk", r))
+        link("c4", "c3", "ya", A.max, m2x)
+        scan(V("ho", 0, 120), V("h0", 0, 120), V("h1", 0, 120), A.mult, A.add)
+        scan(row("u4"), row("m2b"), row("c4"), A.add, A.min)
+        tt(six("g1", -1), three("ho", 2, 20, 20), three("ho", 2, 0, 20), A.subtract)
+        scan(row("u5"), row("m2b"), row("yc"), A.add, A.min)
+        af(six("g1", 1), three("ho", 2, 0, 20), FN.Copy)
         lq, ls = V("ql", K + K * r, 128), V("sl", K + K * r, 128)
         for e in range(4):
             mm(bank(L0 + e, 0, 128), V("qe", 128 * e, 128), V("se", 128 * e, 128), lq, ls,
                ext=[("arr%d" % r, arrivals)] if e == 0 else [])
-        for e in range(5):
-            if e < 4:
-                af(V("dec", K * e, K), bank(L0 + e, K, K), FN.Copy)
-            if e:
-                af(V("fx", FW * (e - 1) + C, K), V("dec", K * (e - 1), K), FN.Copy, off=V("po", 0, 4))
         for e in range(4):
-            af(V("hh", FW * e + C, K), V("fx", FW * e + C, K), FN.Copy, 2.0)
-        scan(row("t4"), row("mm"), row("c4"), A.add, A.min)
-        ta, tb, kk = V("ta", 0, 20), V("tb", 0, 20), V("kk", 0, 20)
-        ts(ta, t4, col(3), A.is_lt, -2.0 ** 25, A.mult)
-        tt(tb, t4, ta, A.max)
-        tt(V("ki", 0, 20), t3, tb, A.min)
-        ts(kk, V("ki", 0, 20), 3, A.bitwise_and)
-        ts(five("h0", 1), kk, -1.0, A.add, 0.5, A.mult, grp=("kk", r))
-        cp(five("h0", 2), kk, grp=("kk", r))
-        scan(V("ho", 0, 100), V("h0", 0, 100), V("h1", 0, 100), A.mult, A.add)
-        cp(V("to", 0, 20), five("ho", 4))
-        to = V("to", 0, 20)
+            af(plane("fx", e, C, K), bank(L0 + e, K, K), FN.Copy)
         for e in range(4):
-            tt(V("hh", FW * e, C), V("fx", FW * e, FW), V(xs, e, C, 4), A.add, to)
+            af(plane("hh", e, C, K), bank(L0 + e, K, K), FN.Copy, 2.0)
+        if r == 0:
+            af(plane("yy", 1), V("xt", 1, C, 4), FN.Copy, 32.0)
+        ts(six("g0", 0), ends("u4"), col(10), A.is_lt, grp=("fl", r))
+        ts(six("g0", 1), ends("u5"), col(10), A.is_lt, grp=("fl", r))
+        scan(V("go", 0, 140), V("g0", 0, 140), V("g1", 0, 140), A.mult, A.add)
+        cp(tab("to"), six("go", 5))
+        to = tab("to")
+        for e in range(4):
+            tt(plane("hh", e), plane("fx", e, 0, FW), V("xn" if r else "xt", e, C, 4), A.add, to)
             if e < 3:
-                af(V("zt", e, C, 4), V("hh", FW * e, FW), FN.Copy, 0.5, off=to)
+                af(V("zt", e, C, 4), plane("hh", e, 0, FW), FN.Copy, 0.5, off=to)
         if last:
             fill(V("tt", 20, 12), 0.0)
-        ts(V("zt", 3, HC, 4), V("hh", FW * 3, FW), 0.5, A.mult, off=V("to", 0, 10))
-        af(V("zt", 3 + 2 * C, HC, 4), V("hh", FW * 3, FW), FN.Copy, 0.5, off=V("to", 10, 10))
+        ts(V("zt", 3, HC, 4), plane("hh", 3, 0, FW), 0.5, A.mult, off=V("to", 0, 10))
+        af(V("zt", 3 + 2 * C, HC, 4), plane("hh", 3, 0, FW), FN.Copy, 0.5, off=V("to", 10, 10))
+        if r == 0:
+            for e in range(2, 4):
+                af(plane("yy", e), V("xt", e, C, 4), FN.Copy, 32.0)
         if last:
-            cp(V("tt", 0, 20), five("ho", 4))
+            cp(V("tt", 0, 20), six("go", 3))
         for h in range(2):
             quant(half("qz", h), half("sz", h), half("zt", h, 4))
             for e in range(4):
@@ -522,20 +605,29 @@ def rank_ops(g, core, T, topo, rank):
                     [V("tr", 0, 32)], [], "ot")
         if r == 0:
             quant(qv, sv, V("vt", 0, 512))
-        lhs = (qv, sv) if last else (qp, sp)
         for h in range(2):
             for e in range(4):
-                y = V("yy", C * e + HC * h, HC)
+                y = plane("yy", e, HC * h, HC)
                 tt(y, bank((L0 + e + 4 * h) % 8, 0, HC), y, A.add)
                 if (h, e) != (1, 3):
                     af(V("xn", 2 * C * h + e, HC, 4), y, FN.Copy, 1.0 / 32, grp=("xn", r, h))
                 if (h, e) == (1, 1):
                     quant(half("qx", 0), half("sx", 0), half("xn", 0, 4))
-                    mm(bank(L0, 0, HC), lhs[0], lhs[1], half("qx", 0), half("sx", 0))
                     if last:
+                        mm(bank(L0, 0, HC), qv, sv, half("qx", 0), half("sx", 0))
                         codes_out("s", 0)
-        ts(V("xn", 2 * C + 3, HC, 4), V("yy", 3 * C + HC, HC), 1.0 / 32, A.mult)
+                    else:
+                        scores(L0, HC)
+                        scores(L0 + 2, HC)
+        if not last:
+            mask(0, L0, 0)
+        ts(V("xn", 2 * C + 3, HC, 4), plane("yy", 3, HC, HC), 1.0 / 32, A.mult)
+        if not last:
+            hold(0, 0)
+            mask(0, L0, 1)
         quant(half("qx", 1), half("sx", 1), half("xn", 1, 4))
+        if not last:
+            hold(0, 1)
 
     mm(bank(L0 + 1, 0, HC), qv, sv, half("qx", 1), half("sx", 1))
     af(half("ys", 0), bank(L0, 0, HC), FN.Copy)

@@ -9,12 +9,12 @@ FRAC = 4096.0
 OFF1 = 512.0
 OFF2 = 16.0
 HUGE = 2.0 ** 80
-CUT1, CUT3 = 160, 96
+CUT1, CUT3 = 224, 128
 TILES = ((0, 320, (9, 0)), (320, 128, (1, 2)), (448, 128, (3, 4)), (576, 192, (5, 6)), (768, 256, (7, 8)))
 CTW = 1024
-ACT_EARLY = ((4, 0), (3, 0), (4, 1), (3, 1))
+ACT_EARLY = ((4, 0), (3, 0), (2, 0), (4, 1), (3, 1))
 ACT_LATE = ((9, 0), (8, 0), (9, 1), (8, 1), (7, 0), (7, 1))
-VEC_ROWS = ((1, 0), (1, 1), (2, 0), (2, 1), (5, 0), (5, 1), (6, 0), (6, 1))
+VEC_ROWS = ((1, 0), (1, 1), (2, 1), (5, 0), (5, 1), (6, 0), (6, 1))
 RS = 96
 
 F32, BF, I32, U16, MX, U8 = "float32", "bfloat16", "int32", "uint16", "float8_e4m3fn_x4", "uint8"
@@ -55,7 +55,7 @@ for _n in ("mm hm hi hd ov key a0 a1 s1 xa xb c1 t1 u1").split():
     SCRATCH[_n] = _sb(C, F32)
 for _n in ("rr", "r16", "mk", "rs"):
     SCRATCH[_n] = _sb(HC, BF)
-for _n in ("n0 c2 e1 c3 c4 ya yb yc m2b u2 u3 u4 u5").split():
+for _n in ("n0 c2 e1 c3 c4 ya yb yc m2b u2 u3 u4 u5 u6 fl").split():
     SCRATCH[_n] = _sb(CW, BF)
 POOL = ["p%d" % i for i in range(110)]
 SEMAPHORES = POOL + ["arr%d" % r for r in range(R)] + ["mid%d" % r for r in range(R)] + ["sent"]
@@ -272,8 +272,9 @@ def rank_ops(g, core, T, topo, rank):
 
     m0, m1, m2, m2x = V("mvo", 0, 20), V("mvo", 20, 20), V("mvo", 40, 20), V("m2o", 0, 20)
 
-    def link(out, win, in1, op, off):
-        tt(row(out), row(win, 0, CW if off == m2x else C), row(in1), op, off)
+    def link(out, win, in1, op, off, a=0, b=C):
+        tt(row(out, a, b - a), row(win, 0, CW if off == m2x else C), row(in1, a, b - a), op,
+           V(off[0], off[1] + a // 16, (b - a) // 16))
 
     later = []
 
@@ -420,25 +421,26 @@ def rank_ops(g, core, T, topo, rank):
 
     scores(L0, HC)
     scores(L0 + 2, HC)
+    mask(0, L0, 0)
     quant(half("qx", 1), half("sx", 1), half("xt", 1, 4))
-    for p in range(2):
-        mask(0, L0, p)
-    for p in range(2):
-        hold(0, p)
+    hold(0, 0)
 
     for r in range(R):
         last = r == R - 1
         for p in range(2):
             for b in (SV, SA):
                 mm(bank(b + p), V("qp", 128 * p, 128), V("sp", 128 * p, 128), row("qx"), row("sx"))
-        arows(ACT_EARLY, L0 + 2)
+        mask(0, L0, 1)
         inner(0, L0, 0)
+        hold(0, 1)
+        arows(ACT_EARLY, L0 + 2)
         mask(1, SV, 0)
         inner(0, L0, 1)
         hold(1, 0)
         mask(1, SV, 1)
         inner(1, SV, 0)
         hold(1, 1)
+        vrows(VEC_ROWS[:4], SV)
         arows(ACT_LATE, SA)
         if r == 0:
             ts(V("r16", 0, HC), V("r16", 0, HC), col(8), A.is_equal)
@@ -449,69 +451,73 @@ def rank_ops(g, core, T, topo, rank):
         inner(1, SV, 1)
         if r == 0:
             ts(V("kt", 0, 512), V("g8", 0, 512), col(0), A.is_equal)
-        vrows(VEC_ROWS[:4], SV)
+        pack(1)
         if r == 0:
             quant(qk, sk, V("kt", 0, 512))
         for p in range(2):
             scan(V("cm", 176 * p + 16, HC), lane(0, p, 0, 2), lane(0, p, 1, 2), A.add, A.add, -128.0)
-        pack(1)
         vrows(VEC_ROWS[4:], SV)
         pack(2)
-        pack(0)
-        for t in range(3):
-            count(t, r)
         if r == 0:
             ts(tab("cs"), tab("cs"), 1 + 1 / FRAC, A.mult, col(6), A.add)
         for p in range(2):
             tt(V("rd", p, 10, 2), V("cm", 176 * p + 15, 10, 16), V("cm", 176 * p + 31, 10, 16), A.subtract, grp=("rd", r))
         vsums(VEC_ROWS[:4], r)
         tt(tab("re"), tab("rd"), tab("cs"), A.add)
+        pack(0)
         vsums(VEC_ROWS[4:], r)
         pack(3)
-        count(3, r)
+        for t in range(4):
+            count(t, r)
         tt(V("hi", 0, 20, 16), tab("re"), V("rb", RS - 1, 20, RS), A.subtract)
         pack(4)
         count(4, r)
-        scan(row("hd"), row("hm"), row("hi"), A.mult, A.add)
-        gap()
-        put("v", "tr", lambda: vec.transpose(T.ov[:], T.hd[:]), [row("hd")], [row("ov")])
+        for h in range(2):
+            scan(half("hd", h), half("hm", h), half("hi", h), A.mult, A.add)
+        for h in range(2):
+            put("v", "tr", lambda h=h: vec.transpose(ap(half("ov", h)), ap(half("hd", h))), [half("hd", h)], [half("ov", h)])
 
         def sums(m):
             af(V("junk", C * m, C), row("key"), FN.Relu, -1.0, V("bias", m, 1), acc=V("gs", m, 1), grp=("gs", r))
 
+        for h in range(2):
+            tt(half("key", h), bank(PV, HC * h, HC), half("ov", h), A.add)
+            af(half("s1", h), half("key", h), FN.Relu, -1024.0, 1024 * 256.5)
+        scan(half("t1", 0), half("mm", 0), half("key", 0), A.add, A.min)
         gap()
-        tt(row("key"), bank(PV), row("ov"), A.add)
-        gap()
-        af(row("s1"), row("key"), FN.Relu, -1024.0, 1024 * 256.5)
-        scan(row("t1"), row("mm"), row("key"), A.add, A.min)
-        tt(row("a0"), row("key"), row("s1"), A.min)
+        for h in range(2):
+            tt(half("a0", h), half("key", h), half("s1", h), A.min)
         sums(0)
         sums(1)
         af(row("xa", CUT1, C - CUT1), row("a0"), FN.Identity, 1.0, -0.25, off=V("mvo", CUT1 // 16, 20 - CUT1 // 16))
         af(row("a1"), row("a0"), FN.Identity, 1.0, 0.25)
         for m in range(2, 5):
             sums(m)
-        gap()
+        scan(half("t1", 1), half("mm", 1), half("key", 1), A.add, A.min)
         ts(row("xa", 0, CUT1), row("a0"), -0.25, A.add, off=V("mvo", 0, CUT1 // 16))
         gap(2)
-        link("xb", "a0", "xa", A.min, m1)
-        gap()
-        link("c1", "a1", "xb", A.min, m2)
-        gap()
-        ts(row("n0"), row("c1"), 0.5, A.is_ge, 7.0, A.mult)
+        for a, b in ((CUT1, C), (0, CUT1)):
+            link("xb", "a0", "xa", A.min, m1, a, b)
+        for a, b in ((CUT1, C), (0, CUT1)):
+            link("c1", "a1", "xb", A.min, m2, a, b)
+        for a, b in ((CUT1, C), (0, CUT1)):
+            ts(row("n0", a, b - a), row("c1", a, b - a), 0.5, A.is_ge, 7.0, A.mult)
         af(row("ya"), row("n0"), FN.Identity, 8.0 / 7, 1.0, off=m0)
+        scan(half("u1", 0), half("mm", 0), half("c1", 0), A.add, A.min)
         tt(V("oa", 0, 4), V("gs", 0, 4), V("gs", 1, 4), A.subtract)
-        scan(row("u1"), row("mm"), row("c1"), A.add, A.min)
+        scan(half("u1", 1), half("mm", 1), half("c1", 1), A.add, A.min)
         tt(V("ob", 0, 4), V("oa", 0, 4), V("bias", 0, 4), A.add)
+        gap()
         ts(tab("f1"), ends("u1"), col(3), A.is_lt, float(C), A.mult)
         ts(V("oo", 0, 4), V("ob", 0, 4), FRAC, A.mult)
+        ts(tab("ki"), ends("u1"), 4.0, A.mult, 1.0, A.add)
         tt(tab("m2"), tab("f1"), mvi(2), A.max)
         for e in range(1, 4):
             af(V("bt", e, K, 4), plane("fx", e), FN.Copy, off=V("oo", 0, 4), grp=("bt", r))
         cp(V("bt", 0, K, 4), plane("fx", 0), off=V("oo", 0, 4))
+        cp(m2x, tab("m2"))
         link("yb", "n0", "ya", A.add, m1)
         quant(V("qb", 128 * r, 128), V("sb", 128 * r, 128), V("bt", 0, 512))
-        cp(m2x, tab("m2"))
         for part in range(2):
             if relays is None:
                 fn = lambda part=part, r=r: write(g, T, topo, core, dst, piece(T, "land", part, r), piece(T, "made", part, r), "arr%d" % r)
@@ -532,11 +538,10 @@ def rank_ops(g, core, T, topo, rank):
         link("c2", "n0", "yb", A.max, m2x)
         af(row("ya", CUT3, C - CUT3), row("c2"), FN.Identity, 1.0, -1.0, off=V("mvo", CUT3 // 16, 20 - CUT3 // 16))
         af(row("e1"), row("c2"), FN.Identity, 1.0, 1.0)
-        ts(tab("ki"), ends("u1"), 4.0, A.mult, 1.0, A.add)
-        ts(row("ya", 0, CUT3), row("c2"), -1.0, A.add, off=V("mvo", 0, CUT3 // 16))
-        scan(row("u2"), row("m2b"), row("c2"), A.add, A.min)
         ts(tab("k1"), tab("ki"), 3, A.bitwise_and)
         gap()
+        ts(row("ya", 0, CUT3), row("c2"), -1.0, A.add, off=V("mvo", 0, CUT3 // 16))
+        scan(row("u2"), row("m2b"), row("c2"), A.add, A.min)
         tt(tab("al"), tab("k1"), tab("f1"), A.subtract)
         gap(2)
         af(tab("kb"), ends("u2"), FN.Relu, -1.0, col(11))
@@ -548,23 +553,28 @@ def rank_ops(g, core, T, topo, rank):
                 afill(six("g0", j), c)
             afill(six("g1", 0), 0.0)
             af(plane("yy", 0), V("xt", 0, C, 4), FN.Copy, 32.0)
-        link("yb", "c2", "ya", A.min, m1)
-        cp(tab("zi", 20), tab("kb"))
-        link("c3", "e1", "yb", A.min, m2x)
+        for a, b in ((0, HC), (HC, C)):
+            link("yb", "c2", "ya", A.min, m1, a, b)
+        for a, b in ((0, HC), (HC, C)):
+            link("c3", "e1", "yb", A.min, m2x, a, b)
         af(row("ya"), row("c3"), FN.Copy, off=m0)
         af(row("yc"), row("c3"), FN.Copy, off=m1)
-
-        scan(row("u3"), row("m2b"), row("c3"), A.add, A.min)
+        scan(half("u3", 0), half("m2b", 0), half("c3", 0), A.add, A.min)
+        cp(tab("zi", 20), tab("kb"))
+        scan(half("u3", 1), half("m2b", 1), half("c3", 1), A.add, A.min)
+        cp(half("c4", 0), row("c3", 0, CW), off=V("m2o", 0, 10))
         tt(tab("zi"), ends("u3"), tab("am"), A.min)
+        cp(half("c4", 1), row("c3", 0, CW), off=V("m2o", 10, 10))
         kk = V("kk", 0, 40)
         ts(kk, V("zi", 0, 40), 3, A.bitwise_and)
+        scan(row("u4"), row("m2b"), row("c4"), A.add, A.min)
         ts(three("h0", 1), kk, -1.0, A.add, 0.5, A.mult, grp=("kk", r))
         cp(three("h0", 2), kk, grp=("kk", r))
-        link("c4", "c3", "ya", A.max, m2x)
+        scan(row("u6"), row("m2b"), row("ya"), A.add, A.min)
         scan(V("ho", 0, 120), V("h0", 0, 120), V("h1", 0, 120), A.mult, A.add)
-        scan(row("u4"), row("m2b"), row("c4"), A.add, A.min)
-        tt(six("g1", -1), three("ho", 2, 20, 20), three("ho", 2, 0, 20), A.subtract)
+        tt(tab("fl"), ends("u4"), ends("u6"), A.max)
         scan(row("u5"), row("m2b"), row("yc"), A.add, A.min)
+        tt(six("g1", -1), three("ho", 2, 20, 20), three("ho", 2, 0, 20), A.subtract)
         af(six("g1", 1), three("ho", 2, 0, 20), FN.Copy)
         lq, ls = V("ql", K + K * r, 128), V("sl", K + K * r, 128)
         for e in range(4):
@@ -576,19 +586,19 @@ def rank_ops(g, core, T, topo, rank):
             af(plane("hh", e, C, K), bank(L0 + e, K, K), FN.Copy, 2.0)
         if r == 0:
             af(plane("yy", 1), V("xt", 1, C, 4), FN.Copy, 32.0)
-        ts(six("g0", 0), ends("u4"), col(10), A.is_lt, grp=("fl", r))
+        ts(six("g0", 0), tab("fl"), col(10), A.is_lt, grp=("fl", r))
         ts(six("g0", 1), ends("u5"), col(10), A.is_lt, grp=("fl", r))
         scan(V("go", 0, 140), V("g0", 0, 140), V("g1", 0, 140), A.mult, A.add)
         cp(tab("to"), six("go", 5))
         to = tab("to")
         for e in range(4):
             tt(plane("hh", e), plane("fx", e, 0, FW), V("xn" if r else "xt", e, C, 4), A.add, to)
-            if e < 3:
-                af(V("zt", e, C, 4), plane("hh", e, 0, FW), FN.Copy, 0.5, off=to)
+            for a, b in (((0, 20),), ((0, 20),), ((0, 16),), ((6, 10), (10, 20)))[e]:
+                af(V("zt", e + 64 * a, 16 * (b - a), 4), plane("hh", e, 0, FW), FN.Copy, 0.5, off=V("to", a, b - a))
+        for e, a, b in ((2, 16, 20), (3, 0, 6)):
+            ts(V("zt", e + 64 * a, 16 * (b - a), 4), plane("hh", e, 0, FW), 0.5, A.mult, off=V("to", a, b - a))
         if last:
             fill(V("tt", 20, 12), 0.0)
-        ts(V("zt", 3, HC, 4), plane("hh", 3, 0, FW), 0.5, A.mult, off=V("to", 0, 10))
-        af(V("zt", 3 + 2 * C, HC, 4), plane("hh", 3, 0, FW), FN.Copy, 0.5, off=V("to", 10, 10))
         if r == 0:
             for e in range(2, 4):
                 af(plane("yy", e), V("xt", e, C, 4), FN.Copy, 32.0)
@@ -609,8 +619,10 @@ def rank_ops(g, core, T, topo, rank):
             for e in range(4):
                 y = plane("yy", e, HC * h, HC)
                 tt(y, bank((L0 + e + 4 * h) % 8, 0, HC), y, A.add)
-                if (h, e) != (1, 3):
+                if e < 3:
                     af(V("xn", 2 * C * h + e, HC, 4), y, FN.Copy, 1.0 / 32, grp=("xn", r, h))
+                if (h, e) == (1, 0):
+                    ts(V("xn", 3, HC, 4), plane("yy", 3, 0, HC), 1.0 / 32, A.mult)
                 if (h, e) == (1, 1):
                     quant(half("qx", 0), half("sx", 0), half("xn", 0, 4))
                     if last:
@@ -624,10 +636,7 @@ def rank_ops(g, core, T, topo, rank):
         ts(V("xn", 2 * C + 3, HC, 4), plane("yy", 3, HC, HC), 1.0 / 32, A.mult)
         if not last:
             hold(0, 0)
-            mask(0, L0, 1)
         quant(half("qx", 1), half("sx", 1), half("xn", 1, 4))
-        if not last:
-            hold(0, 1)
 
     mm(bank(L0 + 1, 0, HC), qv, sv, half("qx", 1), half("sx", 1))
     af(half("ys", 0), bank(L0, 0, HC), FN.Copy)

@@ -9,13 +9,14 @@ FRAC = 4096.0
 OFF1 = 512.0
 OFF2 = 16.0
 HUGE = 2.0 ** 80
-CUT1, CUT3 = 224, 128
-TILES = ((0, 320, (9, 0)), (320, 128, (1, 2)), (448, 128, (3, 4)), (576, 192, (5, 6)), (768, 256, (7, 8)))
+CUT1, CUT2, CUT3, CUT4 = 192, 128, 160, 320
+TILES = ((0, 320, (9, 0)), (320, 128, (1, 2)), (448, 128, (3, 4)), (768, 256, (7, 8)), (576, 192, (5, 6)))
 CTW = 1024
-ACT_EARLY = ((4, 0), (3, 0), (2, 0), (4, 1), (3, 1))
-ACT_LATE = ((9, 0), (8, 0), (9, 1), (8, 1), (7, 0), (7, 1))
-VEC_ROWS = ((1, 0), (1, 1), (2, 1), (5, 0), (5, 1), (6, 0), (6, 1))
-RS = 96
+SOON = 0
+ACT_EARLY = ((4, 0), (4, 1), (3, 0), (3, 1))
+ACT_LATE = ((9, 0), (8, 0), (9, 1), (8, 1), (6, 0), (5, 1))
+VEC_ROWS = ((1, 0), (2, 0), (1, 1), (2, 1), (5, 0), (7, 1), (7, 0), (6, 1))
+RS = 112
 
 F32, BF, I32, U16, MX, U8 = "float32", "bfloat16", "int32", "uint16", "float8_e4m3fn_x4", "uint8"
 
@@ -39,11 +40,11 @@ SCRATCH = {
     "mvi": _sb(60, I32), "mvo": _sb(60, U16), "m2o": _sb(20, U16), "d2": _sb(20, F32),
     "yy": _sb(4 * FW, BF), "fx": _sb(4 * FW, BF), "hh": _sb(4 * FW, F32), "zt": _sb(4 * C, BF),
     "bt": _sb(512, BF), "zero": _sb(512, BF), "ct": _sb(4 * CTW, BF), "et": _sb(520, BF),
-    "kt": _sb(512, BF), "g8": _sb(512, BF), "ys": _sb(C, F32),
-    "pi": _sb(2, I32), "qi": _sb(2, I32), "gi": _sb(2, I32), "ri": _sb(2, I32),
+    "kt": _sb(512, BF), "ys": _sb(C, F32),
+    "pi": _sb(2, I32), "qi": _sb(2, I32), "ri": _sb(2, I32),
     "cols": _sb(16, F32), "sm": _sb(8, F32), "uo": _sb(16, U16), "bias": _sb(8, F32),
     "tt": _sb(32, F32), "tr": _sb(32, F32), "to": _sb(20, U16),
-    "junk": _sb(5 * C, F32),
+    "junk": _sb(5 * CW, F32), "key": _sb(C + 4, F32), "gw": _sb(FW, BF), "gc": _sb(C, BF),
     "gs": _sb(8, F32), "oa": _sb(4, F32), "ob": _sb(4, F32), "oo": _sb(4, U16),
     "f1": _sb(20, F32), "m2": _sb(20, F32), "ki": _sb(20, I32), "k1": _sb(20, I32), "al": _sb(20, F32),
     "am": _sb(20, F32), "kb": _sb(20, F32), "zi": _sb(40, I32), "kk": _sb(40, I32), "sg": _sb(20, F32),
@@ -51,7 +52,7 @@ SCRATCH = {
     "g0": _sb(140, F32), "g1": _sb(140, F32), "go": _sb(140, F32), "hb": _sb(20, BF),
     "ps": ("psum", [128, 512 * 8], F32),
 }
-for _n in ("mm hm hi hd ov key a0 a1 s1 xa xb c1 t1 u1").split():
+for _n in ("mm hm hi hd ov a0 a1 s1 xa xb c1 t1 u1").split():
     SCRATCH[_n] = _sb(C, F32)
 for _n in ("rr", "r16", "mk", "rs"):
     SCRATCH[_n] = _sb(HC, BF)
@@ -283,11 +284,12 @@ def rank_ops(g, core, T, topo, rank):
             if later:
                 later.pop(0)()
 
-    dma("a", lambda: T.ut[:], lambda: T.u[:], [], [V("ut", 0, 512)])
+    dma("s", lambda: T.ut[:], lambda: T.u[:], [], [V("ut", 0, 512)])
     for h in range(2):
         dma("s", lambda h=h: T.xt[:, 2 * C * h:2 * C * h + 2 * C], lambda h=h: T.x[:, 2 * C * h:2 * C * h + 2 * C], [],
             [V("xt", 2 * C * h, 2 * C)])
     dma("s", lambda: T.mvi[:], lambda: T.mv[:], [], [V("mvi", 0, 60)])
+    put("s", "wait", None, [V("xt", 0, 4 * C), V("ut", 0, 512)], [])
     dma("s", lambda: T.qw[:].bitcast(dt.uint8), lambda: T.wc[:], [], [V("qw", 0, 512)], "w")
     dma("s", lambda: T.sw[:], lambda: T.ws[:], [], [V("sw", 0, 512)], "w")
     dma("s", lambda: T.vt[:], lambda: T.v[:], [], [V("vt", 0, 512)])
@@ -301,61 +303,73 @@ def rank_ops(g, core, T, topo, rank):
     iota(V("r16", 0, HC), [[0, HC // 16], [1, 16]], 0, 0, True)
     iota(tab("cs"), [[32, 10], [0, 2]], 32, 0, True)
     iota(V("sm", 0, 8), [[1, 8]], 0, 0, True)
-    iota(V("g8", 0, 512), [[1, 8], [0, 32], [-1, 2]], 0, 0, True)
 
     def afill(out, c, grp=None):
         af(out, V("zero", 0, out[2]), FN.Identity, 1.0, c, grp=grp)
 
+    def unit(e):
+        quant(V("qe", 128 * e, 128), V("se", 128 * e, 128), V("et", 3 - e, 512))
+
     fill(V("zero", 0, 512), 0.0)
-    for a, cnt, blocks in TILES:
-        low = 32 * min(b for b in blocks if b)
-        afill(V("ct", 4 * (a + low), 4 * (cnt - low)), 0.0, "ct0")
-    afill(row("hi"), 0.0)
+    fill(V("kt", 0, 512), 0.0)
+    for a in range(4):
+        for p in range(2):
+            c = 128 * a + 65 * p
+            put("a", "ones", lambda a=a, c=c: act.activation(T.kt[32 * a:32 * a + 32, c:c + 63:2], T.zero[32 * a:32 * a + 32, 0:32],
+                                                             FN.Identity, bias=1.0),
+                [V("zero", 0, 32)], [V("kt", c, 32, 2)], "kt")
     afill(row("hm"), 1.0)
-    for v, c in ((V("n0", C, 16), 7.0), (V("hm", 0, 20, 16), 0.0), (V("e1", C, 16), -1.0), (V("c3", C, 16), 15.0)):
-        afill(v, c)
+    afill(row("hi"), 0.0)
+    afill(V("hm", 0, 20, 16), 0.0)
     cp(V("uo", 0, 16), V("uf", 0, 16))
     ts(V("qi", 0, 2), V("pi", 0, 2), 15, A.bitwise_and)
-    ts(V("gi", 0, 2), V("pi", 0, 2), 5, A.arith_shift_right)
     ts(V("ri", 0, 2), V("pi", 0, 2), 31, A.bitwise_and)
     fill(V("rs", 0, HC), HUGE)
     quant(V("ql", 0, 128), V("sl", 0, 128), V("zero", 0, 512))
     cp(col(8), V("qi", 0, 1))
     cp(col(7), V("ri", 0, 1))
-    ts(col(0), V("gi", 0, 1), 2.0, A.mult)
     ts(col(6), V("ri", 0, 1), 1 / FRAC - 1, A.mult, -32 / FRAC, A.add)
     fill(V("rs", 0, HC // 32, 32), -HUGE)
     fill(V("cm", 15, 2, 176), -128.0)
     fill(V("rb", RS - 1, 2, RS), 0.0)
-    fill(V("bt", 4 * K, 512 - 4 * K), 0.0)
-    for e in range(4):
-        quant(V("qe", 128 * e, 128), V("se", 128 * e, 128), V("et", 3 - e, 512))
-    ts(V("mk", 0, HC), V("rr", 0, HC), col(7), A.not_equal, -HUGE, A.mult)
+    quant(V("qk", 0, 128), V("sk", 0, 128), V("kt", 0, 512))
     quant(V("qu", 0, 128), V("su", 0, 128), V("ut", 0, 512))
-    quant(half("qx", 0), half("sx", 0), half("xt", 0, 4))
+    unit(0)
     for p in range(2):
         put("v", "pick", lambda p=p: vec.tensor_copy(T.qp[:, 128 * p:128 * p + 128].bitcast(dt.uint32),
                                                      T.qu[:].bitcast(dt.uint32).indirect(T.uo[:, 8 * p:8 * p + 8])),
             [V("qu", 0, 128), V("uo", 8 * p, 8)], [V("qp", 128 * p, 128)])
         put("a", "pick", lambda p=p: act.activation(T.sp[:, 128 * p:128 * p + 128], T.su[:].indirect(T.uo[:, 8 * p:8 * p + 8]), FN.Copy),
             [V("su", 0, 128), V("uo", 8 * p, 8)], [V("sp", 128 * p, 128)])
+        if p == 0:
+            quant(half("qx", 0), half("sx", 0), half("xt", 0, 4))
+    ts(V("mk", 0, HC), V("rr", 0, HC), col(7), A.not_equal, -HUGE, A.mult)
+    for a, cnt, blocks in TILES:
+        low = 32 * min(b for b in blocks if b)
+        afill(V("ct", 4 * (a + low), 4 * (cnt - low)), 0.0, "ct0")
+    af(tab("cs"), tab("cs"), FN.Identity, 1 + 1 / FRAC, col(6))
 
-    af(col(1), col(8), FN.Identity, 4.0, 1.0)
-    af(col(3), col(8), FN.Identity, OFF1, 0.5 - 15 * OFF1)
-    af(col(4), col(8), FN.Identity, -OFF1, 15 * OFF1 - 256.5)
-    af(col(5), col(8), FN.Identity, -OFF1, 15 * OFF1 + 128 - 257.0)
-    af(col(10), col(8), FN.Identity, OFF2, 4 - 15 * OFF2)
-    af(col(11), col(8), FN.Identity, OFF2, 9 - 15 * OFF2)
-    af(V("bias", 0, 8), V("sm", 0, 8), FN.Identity, 1.0, col(1))
+    def late_constants():
+        af(col(1), col(8), FN.Identity, 4.0, 1.0)
+        af(col(3), col(8), FN.Identity, OFF1, 0.5 - 15 * OFF1)
+        af(col(4), col(8), FN.Identity, -OFF1, 15 * OFF1 - 256.5)
+        af(col(5), col(8), FN.Identity, -OFF1, 15 * OFF1 + 128 - 257.0)
+        af(col(10), col(8), FN.Identity, OFF2, 4 - 15 * OFF2)
+        af(col(11), col(8), FN.Identity, OFF2, 9 - 15 * OFF2)
+        af(V("bias", 0, 8), V("sm", 0, 8), FN.Identity, 1.0, col(1))
+        af(V("key", C, 4), V("sm", 0, 4), FN.Copy, -1.0)
 
     def mvi(k):
         return V("mvi", 20 * k, 20)
 
     later += [
+        lambda: unit(1),
         lambda: cp(V("mvo", 0, 60), V("mvi", 0, 60)),
         lambda: tt(three("h1", 1, 0, 20), mvi(1), mvi(0), A.subtract),
         lambda: tt(tab("d2"), mvi(2), mvi(1), A.subtract),
+        lambda: unit(2),
         lambda: cp(three("h1", 2, 0, 20), mvi(0)),
+        lambda: fill(V("bt", 4 * K, 512 - 4 * K), 0.0),
         lambda: tt(three("h1", 0, 0, 20), tab("d2"), three("h1", 1, 0, 20), A.subtract),
     ]
 
@@ -421,45 +435,46 @@ def rank_ops(g, core, T, topo, rank):
 
     scores(L0, HC)
     scores(L0 + 2, HC)
-    mask(0, L0, 0)
     quant(half("qx", 1), half("sx", 1), half("xt", 1, 4))
-    hold(0, 0)
+    unit(3)
+    mask(0, L0, 0)
+    mask(0, L0, 1)
+    gap(1)
 
     for r in range(R):
         last = r == R - 1
         for p in range(2):
             for b in (SV, SA):
                 mm(bank(b + p), V("qp", 128 * p, 128), V("sp", 128 * p, 128), row("qx"), row("sx"))
-        mask(0, L0, 1)
-        inner(0, L0, 0)
+        hold(0, 0)
         hold(0, 1)
+        inner(0, L0, 0)
+        vrows(VEC_ROWS[0:1], L0)
         arows(ACT_EARLY, L0 + 2)
+        vrows(VEC_ROWS[1:2], L0)
         mask(1, SV, 0)
         inner(0, L0, 1)
+        vrows(VEC_ROWS[2:3], L0)
         hold(1, 0)
         mask(1, SV, 1)
+        vrows(VEC_ROWS[3:4], L0)
         inner(1, SV, 0)
         hold(1, 1)
-        vrows(VEC_ROWS[:4], SV)
+        vrows(VEC_ROWS[4:5], SV)
         arows(ACT_LATE, SA)
         if r == 0:
             ts(V("r16", 0, HC), V("r16", 0, HC), col(8), A.is_equal)
             for h in range(2):
                 af(half("mm", h), V("r16", 0, HC), FN.Identity, 2.0 ** 26, -OFF1)
-        for e in range(4):
+            late_constants()
+        for e in range(3 if r == 0 else 4):
             af(plane("fx", e), V("xn" if r else "xt", e, C, 4), FN.Copy)
         inner(1, SV, 1)
-        if r == 0:
-            ts(V("kt", 0, 512), V("g8", 0, 512), col(0), A.is_equal)
         pack(1)
-        if r == 0:
-            quant(qk, sk, V("kt", 0, 512))
         for p in range(2):
             scan(V("cm", 176 * p + 16, HC), lane(0, p, 0, 2), lane(0, p, 1, 2), A.add, A.add, -128.0)
-        vrows(VEC_ROWS[4:], SV)
+        vrows(VEC_ROWS[5:], SV)
         pack(2)
-        if r == 0:
-            ts(tab("cs"), tab("cs"), 1 + 1 / FRAC, A.mult, col(6), A.add)
         for p in range(2):
             tt(V("rd", p, 10, 2), V("cm", 176 * p + 15, 10, 16), V("cm", 176 * p + 31, 10, 16), A.subtract, grp=("rd", r))
         vsums(VEC_ROWS[:4], r)
@@ -474,56 +489,101 @@ def rank_ops(g, core, T, topo, rank):
         count(4, r)
         for h in range(2):
             scan(half("hd", h), half("hm", h), half("hi", h), A.mult, A.add)
+        gap()
         for h in range(2):
             put("v", "tr", lambda h=h: vec.transpose(ap(half("ov", h)), ap(half("hd", h))), [half("hd", h)], [half("ov", h)])
+        gap()
 
         def sums(m):
-            af(V("junk", C * m, C), row("key"), FN.Relu, -1.0, V("bias", m, 1), acc=V("gs", m, 1), grp=("gs", r))
+            af(V("junk", CW * m, C + 4 - m), row("key", 0, C + 4 - m), FN.Relu, -1.0, V("bias", m, 1), acc=V("gs", m, 1),
+               grp=("gs", r))
 
         for h in range(2):
             tt(half("key", h), bank(PV, HC * h, HC), half("ov", h), A.add)
             af(half("s1", h), half("key", h), FN.Relu, -1024.0, 1024 * 256.5)
+        gap()
         scan(half("t1", 0), half("mm", 0), half("key", 0), A.add, A.min)
         gap()
         for h in range(2):
             tt(half("a0", h), half("key", h), half("s1", h), A.min)
-        sums(0)
-        sums(1)
-        af(row("xa", CUT1, C - CUT1), row("a0"), FN.Identity, 1.0, -0.25, off=V("mvo", CUT1 // 16, 20 - CUT1 // 16))
-        af(row("a1"), row("a0"), FN.Identity, 1.0, 0.25)
-        for m in range(2, 5):
-            sums(m)
-        scan(half("t1", 1), half("mm", 1), half("key", 1), A.add, A.min)
-        ts(row("xa", 0, CUT1), row("a0"), -0.25, A.add, off=V("mvo", 0, CUT1 // 16))
-        gap(2)
-        for a, b in ((CUT1, C), (0, CUT1)):
-            link("xb", "a0", "xa", A.min, m1, a, b)
-        for a, b in ((CUT1, C), (0, CUT1)):
-            link("c1", "a1", "xb", A.min, m2, a, b)
-        for a, b in ((CUT1, C), (0, CUT1)):
-            ts(row("n0", a, b - a), row("c1", a, b - a), 0.5, A.is_ge, 7.0, A.mult)
-        af(row("ya"), row("n0"), FN.Identity, 8.0 / 7, 1.0, off=m0)
-        scan(half("u1", 0), half("mm", 0), half("c1", 0), A.add, A.min)
-        tt(V("oa", 0, 4), V("gs", 0, 4), V("gs", 1, 4), A.subtract)
-        scan(half("u1", 1), half("mm", 1), half("c1", 1), A.add, A.min)
-        tt(V("ob", 0, 4), V("oa", 0, 4), V("bias", 0, 4), A.add)
-        gap()
-        ts(tab("f1"), ends("u1"), col(3), A.is_lt, float(C), A.mult)
-        ts(V("oo", 0, 4), V("ob", 0, 4), FRAC, A.mult)
-        ts(tab("ki"), ends("u1"), 4.0, A.mult, 1.0, A.add)
-        tt(tab("m2"), tab("f1"), mvi(2), A.max)
-        for e in range(1, 4):
-            af(V("bt", e, K, 4), plane("fx", e), FN.Copy, off=V("oo", 0, 4), grp=("bt", r))
-        cp(V("bt", 0, K, 4), plane("fx", 0), off=V("oo", 0, 4))
-        cp(m2x, tab("m2"))
-        link("yb", "n0", "ya", A.add, m1)
-        quant(V("qb", 128 * r, 128), V("sb", 128 * r, 128), V("bt", 0, 512))
-        for part in range(2):
-            if relays is None:
-                fn = lambda part=part, r=r: write(g, T, topo, core, dst, piece(T, "land", part, r), piece(T, "made", part, r), "arr%d" % r)
+        def first_move(a, b, queue):
+            off = V("mvo", a // 16, (b - a) // 16)
+            if queue == "a":
+                af(row("xa", a, b - a), row("a0"), FN.Identity, 1.0, -0.25, off=off)
             else:
-                fn = lambda part=part, r=r: write(g, T, topo, core, relays[part], piece(T, "mid", part, r), piece(T, "made", part, r), "mid%d" % r)
-            put("g", "send", fn, [V(("qb", "sb")[part], 128 * r, 128)], [])
+                ts(row("xa", a, b - a), row("a0"), -0.25, A.add, off=off)
+
+        def border_list(step):
+            if step == 0:
+                tt(V("oa", 0, 4), V("gs", 0, 4), V("gs", 1, 4), A.subtract)
+            else:
+                ts(V("oo", 0, 4), V("oa", 0, 4), FRAC, A.mult)
+
+        def border_tile():
+            for e in range(4):
+                af(V("bt", e, K, 4), plane("fx", e), FN.Copy, off=V("oo", 0, 4), grp=("bt", r))
+
+        def border_out():
+            quant(V("qb", 128 * r, 128), V("sb", 128 * r, 128), V("bt", 0, 512))
+            for part in range(2):
+                to, where, sem = (dst, "land", "arr%d" % r) if relays is None else (relays[part], "mid", "mid%d" % r)
+                put("g", "send", lambda to=to, where=where, sem=sem, part=part, r=r: write(
+                    g, T, topo, core, to, piece(T, where, part, r), piece(T, "made", part, r), sem),
+                    [V(("qb", "sb")[part], 128 * r, 128)], [])
+
+        soon = r < SOON
+        cut = HC if soon else CUT1
+        for m in range(5 if soon else 2):
+            sums(m)
+        if not soon:
+            first_move(cut, C, "a")
+        af(row("a1"), row("a0"), FN.Identity, 1.0, 0.25)
+        for m in range(5 if soon else 2, 5):
+            sums(m)
+        if r == 0:
+            af(plane("fx", 3), V("xt", 3, C, 4), FN.Copy)
+            for v, c in ((V("n0", C, 16), 7.0), (V("e1", C, 16), -1.0), (V("c3", C, 16), 15.0)):
+                afill(v, c)
+        scan(half("t1", 1), half("mm", 1), half("key", 1), A.add, A.min)
+        gap()
+        if soon:
+            first_move(cut, C, "v")
+        first_move(0, cut, "v")
+        gap()
+        for a, b in ((cut, C), (0, cut)):
+            link("xb", "a0", "xa", A.min, m1, a, b)
+        if soon:
+            border_list(0)
+        link("c1", "a1", "xb", A.min, m2, cut, C)
+        if soon:
+            border_list(1)
+            border_tile()
+        link("c1", "a1", "xb", A.min, m2, 0, cut)
+        ts(row("n0", cut, C - cut), row("c1", cut, C - cut), 0.5, A.is_ge, 7.0, A.mult)
+        if not soon:
+            border_list(0)
+        ts(row("n0", 0, cut), row("c1", 0, cut), 0.5, A.is_ge, 7.0, A.mult)
+        af(row("ya", CUT2, C - CUT2), row("n0"), FN.Identity, 8.0 / 7, 1.0, off=V("mvo", CUT2 // 16, 20 - CUT2 // 16))
+        if not soon:
+            border_list(1)
+            border_tile()
+        scan(row("u1"), row("mm"), row("c1"), A.add, A.min)
+        ts(row("ya", 0, CUT2), row("n0"), 8.0 / 7, A.mult, 1.0, A.add, off=V("mvo", 0, CUT2 // 16))
+        ts(tab("f1"), ends("u1"), col(3), A.is_lt, float(C), A.mult)
+        if soon:
+            border_out()
+            tt(tab("m2"), tab("f1"), mvi(2), A.max)
+        ts(tab("ki"), ends("u1"), 4.0, A.mult, 1.0, A.add)
+        gap()
+        link("yb", "n0", "ya", A.add, m1, 0, HC)
+        if soon:
+            cp(m2x, tab("m2"))
+        else:
+            tt(tab("m2"), tab("f1"), mvi(2), A.max)
+        link("yb", "n0", "ya", A.add, m1, HC, C)
+        if not soon:
+            cp(m2x, tab("m2"))
+            border_out()
         af(tab("cb"), ends("t1"), FN.Identity, 1.0, col(5))
         af(tab("sg"), ends("t1"), FN.Sign, 1.0, col(4))
         af(six("g1", 2), tab("cb"), FN.Relu, 1.0, -128.0)
@@ -535,13 +595,15 @@ def rank_ops(g, core, T, topo, rank):
         if r == 0:
             for h in range(2):
                 af(half("m2b", h), V("r16", 0, HC), FN.Identity, 2.0 ** 26, -OFF2)
-        link("c2", "n0", "yb", A.max, m2x)
+        for a, b in ((0, HC), (HC, C)):
+            link("c2", "n0", "yb", A.max, m2x, a, b)
         af(row("ya", CUT3, C - CUT3), row("c2"), FN.Identity, 1.0, -1.0, off=V("mvo", CUT3 // 16, 20 - CUT3 // 16))
         af(row("e1"), row("c2"), FN.Identity, 1.0, 1.0)
+        scan(half("u2", 0), half("m2b", 0), half("c2", 0), A.add, A.min)
         ts(tab("k1"), tab("ki"), 3, A.bitwise_and)
         gap()
         ts(row("ya", 0, CUT3), row("c2"), -1.0, A.add, off=V("mvo", 0, CUT3 // 16))
-        scan(row("u2"), row("m2b"), row("c2"), A.add, A.min)
+        scan(half("u2", 1), half("m2b", 1), half("c2", 1), A.add, A.min)
         tt(tab("al"), tab("k1"), tab("f1"), A.subtract)
         gap(2)
         af(tab("kb"), ends("u2"), FN.Relu, -1.0, col(11))
@@ -552,90 +614,110 @@ def rank_ops(g, core, T, topo, rank):
             for j, c in ((-1, 0.0), (3, 1.0), (4, 1.0), (5, 1.0)):
                 afill(six("g0", j), c)
             afill(six("g1", 0), 0.0)
-            af(plane("yy", 0), V("xt", 0, C, 4), FN.Copy, 32.0)
+            afill(V("tt", 20, 12), 0.0)
+            for e in range(2):
+                af(plane("yy", e), V("xt", e, C, 4), FN.Copy, 32.0)
         for a, b in ((0, HC), (HC, C)):
             link("yb", "c2", "ya", A.min, m1, a, b)
         for a, b in ((0, HC), (HC, C)):
             link("c3", "e1", "yb", A.min, m2x, a, b)
         af(row("ya"), row("c3"), FN.Copy, off=m0)
+        if CUT4 < C:
+            af(row("c4", CUT4, C - CUT4), row("c3", 0, CW), FN.Copy, off=V("m2o", CUT4 // 16, 20 - CUT4 // 16))
         af(row("yc"), row("c3"), FN.Copy, off=m1)
+        if r == 0:
+            for e in range(2, 4):
+                af(plane("yy", e), V("xt", e, C, 4), FN.Copy, 32.0)
         scan(half("u3", 0), half("m2b", 0), half("c3", 0), A.add, A.min)
         cp(tab("zi", 20), tab("kb"))
         scan(half("u3", 1), half("m2b", 1), half("c3", 1), A.add, A.min)
         cp(half("c4", 0), row("c3", 0, CW), off=V("m2o", 0, 10))
         tt(tab("zi"), ends("u3"), tab("am"), A.min)
-        cp(half("c4", 1), row("c3", 0, CW), off=V("m2o", 10, 10))
+        cp(row("c4", HC, CUT4 - HC), row("c3", 0, CW), off=V("m2o", 10, (CUT4 - HC) // 16))
         kk = V("kk", 0, 40)
         ts(kk, V("zi", 0, 40), 3, A.bitwise_and)
-        scan(row("u4"), row("m2b"), row("c4"), A.add, A.min)
+        scan(row("u6"), row("m2b"), row("ya"), A.add, A.min)
         ts(three("h0", 1), kk, -1.0, A.add, 0.5, A.mult, grp=("kk", r))
         cp(three("h0", 2), kk, grp=("kk", r))
-        scan(row("u6"), row("m2b"), row("ya"), A.add, A.min)
+        scan(row("u4"), row("m2b"), row("c4"), A.add, A.min)
         scan(V("ho", 0, 120), V("h0", 0, 120), V("h1", 0, 120), A.mult, A.add)
-        tt(tab("fl"), ends("u4"), ends("u6"), A.max)
         scan(row("u5"), row("m2b"), row("yc"), A.add, A.min)
+        tt(tab("fl"), ends("u4"), ends("u6"), A.max)
         tt(six("g1", -1), three("ho", 2, 20, 20), three("ho", 2, 0, 20), A.subtract)
         af(six("g1", 1), three("ho", 2, 0, 20), FN.Copy)
         lq, ls = V("ql", K + K * r, 128), V("sl", K + K * r, 128)
-        for e in range(4):
+        for e in (0, 3, 1, 2):
             mm(bank(L0 + e, 0, 128), V("qe", 128 * e, 128), V("se", 128 * e, 128), lq, ls,
                ext=[("arr%d" % r, arrivals)] if e == 0 else [])
-        for e in range(4):
+        for e in (0, 3, 1, 2):
             af(plane("fx", e, C, K), bank(L0 + e, K, K), FN.Copy)
-        for e in range(4):
-            af(plane("hh", e, C, K), bank(L0 + e, K, K), FN.Copy, 2.0)
-        if r == 0:
-            af(plane("yy", 1), V("xt", 1, C, 4), FN.Copy, 32.0)
-        ts(six("g0", 0), tab("fl"), col(10), A.is_lt, grp=("fl", r))
+        af(V("gw", C, K), bank(L0 + 3, K, K), FN.Copy, 0.5)
         ts(six("g0", 1), ends("u5"), col(10), A.is_lt, grp=("fl", r))
+        ts(six("g0", 0), tab("fl"), col(10), A.is_lt, grp=("fl", r))
         scan(V("go", 0, 140), V("g0", 0, 140), V("g1", 0, 140), A.mult, A.add)
         cp(tab("to"), six("go", 5))
         to = tab("to")
-        for e in range(4):
+
+        def zrun(e, h):
+            return V("zt", e + 2 * C * h, HC, 4)
+
+        for e in range(2):
+            af(plane("hh", e, C, K), bank(L0 + e, K, K), FN.Copy, 2.0)
+        af(row("gw"), plane("fx", 3, 0, FW), FN.Copy, 0.5, off=to)
+        af(plane("hh", 2, C, K), bank(L0 + 2, K, K), FN.Copy, 2.0)
+        af(row("gc"), row("gw"), FN.Copy)
+        for e in range(3):
             tt(plane("hh", e), plane("fx", e, 0, FW), V("xn" if r else "xt", e, C, 4), A.add, to)
-            for a, b in (((0, 20),), ((0, 20),), ((0, 16),), ((6, 10), (10, 20)))[e]:
-                af(V("zt", e + 64 * a, 16 * (b - a), 4), plane("hh", e, 0, FW), FN.Copy, 0.5, off=V("to", a, b - a))
-        for e, a, b in ((2, 16, 20), (3, 0, 6)):
-            ts(V("zt", e + 64 * a, 16 * (b - a), 4), plane("hh", e, 0, FW), 0.5, A.mult, off=V("to", a, b - a))
-        if last:
-            fill(V("tt", 20, 12), 0.0)
-        if r == 0:
-            for e in range(2, 4):
-                af(plane("yy", e), V("xt", e, C, 4), FN.Copy, 32.0)
-        if last:
-            cp(V("tt", 0, 20), six("go", 3))
+        af(V("zt", 0, C, 4), plane("hh", 0, 0, FW), FN.Copy, 0.5, off=to)
+        for e, h in ((1, 0), (1, 1), (2, 1)):
+            af(zrun(e, h), plane("hh", e, 0, FW), FN.Copy, 0.5, off=V("to", 10 * h, 10))
+        tt(zrun(3, 0), V("gw", 0, FW), half("gc", 0), A.add, V("to", 0, 10))
+        ts(zrun(2, 0), plane("hh", 2, 0, FW), 0.5, A.mult, off=V("to", 0, 10))
+        tt(V("zt", 3 + 2 * C, 64, 4), V("gw", 0, FW), V("gc", HC, 64), A.add, V("to", 10, 4))
         for h in range(2):
             quant(half("qz", h), half("sz", h), half("zt", h, 4))
-            for e in range(4):
+            for e in ((0, 1, 2, 3), (3, 0, 1, 2))[h]:
                 mm(bank((L0 + e + 4 * h) % 8, 0, HC), V("qw", 128 * e, 128), V("sw", 128 * e, 128), half("qz", h), half("sz", h))
+            if h == 0:
+                tt(V("zt", 3 + 2 * C + 256, 96, 4), V("gw", 0, FW), V("gc", HC + 64, 96), A.add, V("to", 14, 6))
+                if r == 0:
+                    quant(qv, sv, V("vt", 0, 512))
+                if last:
+                    af(V("tt", 0, 20), six("go", 3), FN.Copy)
+                    put("v", "tr", lambda: vec.transpose(T.tr[:], T.tt[:]), [V("tt", 0, 32)], [V("tr", 0, 32)])
+                    for k in range(8):
+                        dma("s", lambda k=k: T.ot[k, :],
+                            lambda k=k: T.tr[32 * (k // 2):32 * (k // 2) + 20, 16 * (k % 2):16 * (k % 2) + 16],
+                            [V("tr", 0, 32)], [], "ot")
+        def add(h, e):
+            y = plane("yy", e, HC * h, HC)
+            tt(y, bank((L0 + e + 4 * h) % 8, 0, HC), y, A.add)
+            if e < 3 and not (last and (h, e) == (1, 2)):
+                af(V("xn", 2 * C * h + e, HC, 4), y, FN.Copy, 1.0 / 32, grp=("xn", r, h))
+
+        def cast(h, e=3):
+            ts(V("xn", 2 * C * h + e, HC, 4), plane("yy", e, HC * h, HC), 1.0 / 32, A.mult)
+
+        for e in range(4):
+            add(0, e)
+        add(1, 3)
+        cast(0)
+        add(1, 0)
+        quant(half("qx", 0), half("sx", 0), half("xn", 0, 4))
         if last:
-            put("v", "tr", lambda: vec.transpose(T.tr[:], T.tt[:]), [V("tt", 0, 32)], [V("tr", 0, 32)])
-            for k in range(8):
-                dma("s", lambda k=k: T.ot[k, :], lambda k=k: T.tr[32 * (k // 2):32 * (k // 2) + 20, 16 * (k % 2):16 * (k % 2) + 16],
-                    [V("tr", 0, 32)], [], "ot")
-        if r == 0:
-            quant(qv, sv, V("vt", 0, 512))
-        for h in range(2):
-            for e in range(4):
-                y = plane("yy", e, HC * h, HC)
-                tt(y, bank((L0 + e + 4 * h) % 8, 0, HC), y, A.add)
-                if e < 3:
-                    af(V("xn", 2 * C * h + e, HC, 4), y, FN.Copy, 1.0 / 32, grp=("xn", r, h))
-                if (h, e) == (1, 0):
-                    ts(V("xn", 3, HC, 4), plane("yy", 3, 0, HC), 1.0 / 32, A.mult)
-                if (h, e) == (1, 1):
-                    quant(half("qx", 0), half("sx", 0), half("xn", 0, 4))
-                    if last:
-                        mm(bank(L0, 0, HC), qv, sv, half("qx", 0), half("sx", 0))
-                        codes_out("s", 0)
-                    else:
-                        scores(L0, HC)
-                        scores(L0 + 2, HC)
-        if not last:
+            mm(bank(L0, 0, HC), qv, sv, half("qx", 0), half("sx", 0))
+            codes_out("s", 0)
+        else:
+            scores(L0, HC)
+            scores(L0 + 2, HC)
+        add(1, 1)
+        add(1, 2)
+        cast(1)
+        if last:
+            cast(1, 2)
+        else:
             mask(0, L0, 0)
-        ts(V("xn", 2 * C + 3, HC, 4), plane("yy", 3, HC, HC), 1.0 / 32, A.mult)
-        if not last:
-            hold(0, 0)
+            mask(0, L0, 1)
         quant(half("qx", 1), half("sx", 1), half("xn", 1, 4))
 
     mm(bank(L0 + 1, 0, HC), qv, sv, half("qx", 1), half("sx", 1))

import math
from concourse.mybir import dt, AluOpType, ActivationFunctionType

C, K, R = 320, 64, 3
HC = C // 2
FW = C + K
CW = C + 16
FRAC = 4096.0
OFF1 = 512.0
OFF2 = 16.0
HUGE = 2.0 ** 80
CUT1, CUT2, CUT3, CUT4 = 192, 128, 160, 320
TILES = ((0, 320, (9, 0)), (320, 128, (1, 2)), (448, 128, (3, 4)), (768, 256, (7, 8)), (576, 192, (5, 6)))
CTW = 1024
SOON = 0
ACT_EARLY = ((4, 0), (4, 1), (3, 0), (3, 1))
ACT_LATE = ((9, 0), (8, 0), (9, 1), (8, 1), (6, 0), (5, 1))
VEC_ROWS = ((1, 0), (2, 0), (1, 1), (2, 1), (5, 0), (7, 1), (7, 0), (6, 1))
RS = 112

F32, BF, I32, U16, MX, U8 = "float32", "bfloat16", "int32", "uint16", "float8_e4m3fn_x4", "uint8"


def _sb(n, d):
    return ("sbuf", [128, n], d)


SCRATCH = {
    "xt": _sb(4 * C, BF), "xn": _sb(4 * C, BF), "ut": _sb(512, BF), "vt": _sb(512, BF),
    "qu": _sb(128, MX), "su": _sb(128, U8), "qp": _sb(256, MX), "sp": _sb(256, U8),
    "vv": _sb(2 * C, F32), "d1": _sb(2 * C, F32), "rb": _sb(20 * RS, F32), "cm": _sb(2 * 176, BF),
    "rd": _sb(20, F32), "re": _sb(20, F32), "cs": _sb(20, F32), "uf": _sb(16, F32), "cb": _sb(20, BF),
    "qv": _sb(128, MX), "sv": _sb(128, U8), "qx": _sb(C, MX), "sx": _sb(C, U8),
    "qw": _sb(512, MX), "sw": _sb(512, U8), "qz": _sb(C, MX), "sz": _sb(C, U8),
    "qk": _sb(128, MX), "sk": _sb(128, U8), "qe": _sb(512, MX), "se": _sb(512, U8),
    "qc": _sb(CTW, MX), "sc": _sb(CTW, U8),
    "qb": _sb(128 * R, MX), "sb": _sb(128 * R, U8),
    "qr": _sb(K * R, MX), "sr": _sb(K * R, U8),
    "ql": _sb(128 + K * R, MX), "sl": _sb(128 + K * R, U8),
    "mvi": _sb(60, I32), "mvo": _sb(60, U16), "m2o": _sb(20, U16), "d2": _sb(20, F32),
    "yy": _sb(4 * FW, BF), "fx": _sb(4 * FW, BF), "hh": _sb(4 * FW, F32), "zt": _sb(4 * C, BF),
    "bt": _sb(512, BF), "zero": _sb(512, BF), "ct": _sb(4 * CTW, BF), "et": _sb(520, BF),
    "kt": _sb(512, BF), "ys": _sb(C, F32),
    "pi": _sb(2, I32), "qi": _sb(2, I32), "ri": _sb(2, I32),
    "cols": _sb(16, F32), "sm": _sb(8, F32), "uo": _sb(16, U16), "bias": _sb(8, F32),
    "tt": _sb(32, F32), "tr": _sb(32, F32), "to": _sb(20, U16),
    "junk": _sb(5 * CW, F32), "key": _sb(C + 4, F32), "gw": _sb(FW, BF), "gc": _sb(C, BF),
    "gs": _sb(8, F32), "oa": _sb(4, F32), "ob": _sb(4, F32), "oo": _sb(4, U16),
    "f1": _sb(20, F32), "m2": _sb(20, F32), "ki": _sb(20, I32), "k1": _sb(20, I32), "al": _sb(20, F32),
    "am": _sb(20, F32), "kb": _sb(20, F32), "zi": _sb(40, I32), "kk": _sb(40, I32), "sg": _sb(20, F32),
    "h0": _sb(120, F32), "h1": _sb(120, F32), "ho": _sb(120, F32),
    "g0": _sb(140, F32), "g1": _sb(140, F32), "go": _sb(140, F32), "hb": _sb(20, BF),
    "ps": ("psum", [128, 512 * 8], F32),
}
for _n in ("mm hm hi hd ov a0 a1 s1 xa xb c1 t1 u1").split():
    SCRATCH[_n] = _sb(C, F32)
for _n in ("rr", "r16", "mk", "rs"):
    SCRATCH[_n] = _sb(HC, BF)
for _n in ("n0 c2 e1 c3 c4 ya yb yc m2b u2 u3 u4 u5 u6 fl").split():
    SCRATCH[_n] = _sb(CW, BF)
POOL = ["p%d" % i for i in range(110)]
SEMAPHORES = POOL + ["arr%d" % r for r in range(R)] + ["mid%d" % r for r in range(R)] + ["sent"]

A = AluOpType
FN = ActivationFunctionType


def V(name, a, n, step=1):
    return (name, a, n, step)


def bank(b, a=0, n=C):
    return ("ps", 512 * b + a, n, 1)


def _meet(u, v):
    if u[0] != v[0]:
        return False
    if u[0] == "ps":
        return u[1] // 512 == v[1] // 512
    if u[1] + (u[2] - 1) * u[3] < v[1] or v[1] + (v[2] - 1) * v[3] < u[1]:
        return False
    return (u[1] - v[1]) % max(math.gcd(u[3] * (u[2] > 1), v[3] * (v[2] > 1)), 1) == 0


def road(T, topo, r):
    n = len(T.cores)
    src, dst = T.cores[(r + 1) % n], T.cores[r]
    if topo.may_write(src, dst):
        return src, None, dst
    able = [c for c in topo.cores_of(src) if c != src and T.rank_of(c) is None and topo.may_write(c, dst)]
    able.sort(key=lambda c: topo.die(c) != topo.die(src))
    return src, able[:2], dst


def piece(T, where, part, r):
    names, a = {"made": (("qb", "sb"), 128 * r), "mid": (("qr", "sr"), K * r), "land": (("ql", "sl"), 128 + K * r)}[where]
    v = T[names[part]][:, a:a + K]
    return v.bitcast(dt.uint8) if part == 0 else v


def write(g, T, topo, me, to, out, in_, sem):
    rid, pid = topo.addr(to, me)
    return g.remote_dma(out, in_, T.sem[sem], T.sem.sent, pid, rid, topo.mask(me, to))


def relay_program(g, core, T, topo, src, dst, part):
    for r in range(R):
        g.wait_ge(T.sem["mid%d" % r], len(topo.engines(src, core)))
        write(g, T, topo, core, dst, piece(T, "land", part, r), piece(T, "mid", part, r), "arr%d" % r)
    g.wait_ge(T.sem.sent, R * len(topo.engines(core, dst)))


def run(ops, queues, T):
    known = dict((q, 0) for q in queues)
    members = {}
    for i, o in enumerate(ops):
        members.setdefault(o["grp"] if o["grp"] is not None else ("op", i), []).append(i)
    gid = [o["grp"] if o["grp"] is not None else ("op", i) for i, o in enumerate(ops)]
    at_issue, waits, needed = [], [], set()
    touch = {}
    for i, o in enumerate(ops):
        q = o["q"]
        deps = set(o["after"])
        for v, w in [(v, False) for v in o["r"]] + [(v, True) for v in o["w"]]:
            for j, u, wj in touch.get(v[0], []):
                if known[q] >> j & 1 or not _meet(u, v):
                    continue
                if v[0] == "ps" and not w and not wj and ops[j]["q"] == q:
                    continue
                if w or wj or v[0] == "ps":
                    if not (o["acc"] and gid[j] == gid[i]):
                        deps.add(j)
        mine = []
        for j in sorted(deps, reverse=True):
            if known[q] >> j & 1:
                continue
            assert members[gid[j]][-1] < i, (o["name"], ops[j]["name"])
            mine.append(gid[j])
            needed.add(gid[j])
            for k in members[gid[j]]:
                known[q] |= (1 << k) | at_issue[k]
        waits.append(mine)
        at_issue.append(known[q])
        for v in o["r"]:
            touch.setdefault(v[0], []).append((i, v, False))
        for v in o["w"]:
            touch.setdefault(v[0], []).append((i, v, True))
    count = dict((s, 0) for s in POOL)
    users = dict((s, 0) for s in POOL)
    sem_of = {}
    for i, o in enumerate(ops):
        eng = queues[o["q"]]
        for gk in waits[i]:
            s, n = sem_of[gk]
            eng.wait_ge(T.sem[s], n)
        for s, n in o["ext"]:
            eng.wait_ge(T.sem[s], n)
        if o["fn"] is None:
            continue
        ins = o["fn"]()
        gk = gid[i]
        if gk in needed:
            step = 16 if o["dma"] else 1
            if gk not in sem_of:
                free = [s for s in POOL if users[s] & ~at_issue[i] == 0 and not (o["dma"] and count[s])]
                s = free[0]
                count[s] += step * len(members[gk])
                for k in members[gk]:
                    users[s] |= 1 << k
                if o["dma"]:
                    users[s] |= 1 << len(ops)
                sem_of[gk] = (s, count[s])
            ins.then_inc(T.sem[sem_of[gk][0]], step)


def rank_ops(g, core, T, topo, rank):
    ops = []
    vec, act, pe, sy = g.vector, g.scalar, g.tensor, g.sync

    def ap(v):
        if v[3] == 1:
            return T[v[0]][:, v[1]:v[1] + v[2]]
        return T[v[0]][:, v[1]:v[1] + (v[2] - 1) * v[3] + 1:v[3]]

    def put(q, name, fn, r, w, grp=None, dma=False, acc=False, ext=(), after=()):
        ops.append({"q": q, "name": name, "fn": fn, "r": list(r), "w": list(w), "grp": grp, "dma": dma, "acc": acc,
                    "ext": list(ext), "after": list(after)})
        return len(ops) - 1

    def src(v, off):
        return ap(v) if off is None else ap(v).indirect(ap(off))

    def views(*xs):
        return [x for x in xs if isinstance(x, tuple)]

    def num(x):
        return ap(x) if isinstance(x, tuple) else x

    def ts(out, in0, s1, op0, s2=None, op1=None, off=None, grp=None):
        if op1 is None:
            fn = lambda: vec.tensor_scalar(ap(out), src(in0, off), num(s1), None, op0)
        else:
            fn = lambda: vec.tensor_scalar(ap(out), src(in0, off), num(s1), num(s2), op0, op1)
        put("v", "ts " + out[0], fn, views(in0, s1, s2, off), [out], grp)

    def tt(out, in0, in1, op, off=None, grp=None):
        put("v", "tt " + out[0], lambda: vec.tensor_tensor(ap(out), src(in0, off), ap(in1), op), views(in0, in1, off), [out], grp)

    def cp(out, in0, off=None, grp=None):
        put("v", "cp " + out[0], lambda: vec.tensor_copy(ap(out), src(in0, off)), views(in0, off), [out], grp)

    def scan(out, d0, d1, op0, op1, first=0.0, grp=None):
        put("v", "scan " + out[0], lambda: vec.tensor_tensor_scan(ap(out), ap(d0), ap(d1), first, op0, op1), [d0, d1], [out], grp)

    def fill(out, c):
        put("v", "fill " + out[0], lambda: vec.memset(ap(out), c), [], [out])

    def quant(q, s, t):
        put("v", "quant " + q[0], lambda: vec.quantize_mx(ap(q), ap(s), ap(t)), [t], [q, s])

    def af(out, in0, func, scale=1.0, bias=0.0, off=None, acc=None, grp=None):
        if acc is not None:
            fn = lambda: act.activation(ap(out), src(in0, off), func, bias=num(bias), scale=scale, accum_out=ap(acc))
        elif func == FN.Copy:
            fn = lambda: act.activation(ap(out), src(in0, off), func, scale=scale)
        else:
            fn = lambda: act.activation(ap(out), src(in0, off), func, bias=num(bias), scale=scale)
        put("a", "act " + out[0], fn, views(in0, bias, off), views(out, acc), grp)

    def mm(out, lq, ls, rq, rs_, start=True, stop=True, grp=None, ext=()):
        put("t", "mm", lambda: pe.matmul_mx(ap(out), ap(lq), ap(ls), ap(rq), ap(rs_), start, stop), [lq, ls, rq, rs_], [out],
            grp, acc=not start, ext=ext)

    def iota(out, pattern, base, cm, small):
        if small:
            fn = lambda: g.iota(ap(out), pattern, base, cm, allow_small_or_imprecise_dtypes=True)
        else:
            fn = lambda: g.iota(ap(out), pattern, base, cm)
        put("g", "iota " + out[0], fn, [], [out])

    stores = []

    def dma(q, out, in0, r, w, grp=None):
        eng = {"s": sy, "a": act}[q]
        i = put(q, "dma", lambda: eng.dma_start(out(), in0()), r, w, grp, dma=True)
        if not w:
            stores.append((q, i))

    def row(name, a=0, n=C):
        return V(name, a, n)

    def col(j):
        return V("cols", j, 1)

    def tab(name, a=0):
        return V(name, a, 20)

    def ends(name):
        return V(name, 15, 20, 16)

    def three(name, j, a=0, n=40):
        return V(name, 3 * a + j, n, 3)

    def six(name, j):
        return V(name, j + 1, 20, 7)

    def half(name, h, wide=1):
        return V(name, HC * wide * h, HC * wide)

    def plane(name, e, a=0, n=C):
        return V(name, FW * e + a, n)

    m0, m1, m2, m2x = V("mvo", 0, 20), V("mvo", 20, 20), V("mvo", 40, 20), V("m2o", 0, 20)

    def link(out, win, in1, op, off, a=0, b=C):
        tt(row(out, a, b - a), row(win, 0, CW if off == m2x else C), row(in1, a, b - a), op,
           V(off[0], off[1] + a // 16, (b - a) // 16))

    later = []

    def gap(n=1):
        for _ in range(n):
            if later:
                later.pop(0)()

    dma("s", lambda: T.ut[:], lambda: T.u[:], [], [V("ut", 0, 512)])
    for h in range(2):
        dma("s", lambda h=h: T.xt[:, 2 * C * h:2 * C * h + 2 * C], lambda h=h: T.x[:, 2 * C * h:2 * C * h + 2 * C], [],
            [V("xt", 2 * C * h, 2 * C)])
    dma("s", lambda: T.mvi[:], lambda: T.mv[:], [], [V("mvi", 0, 60)])
    put("s", "wait", None, [V("xt", 0, 4 * C), V("ut", 0, 512)], [])
    dma("s", lambda: T.qw[:].bitcast(dt.uint8), lambda: T.wc[:], [], [V("qw", 0, 512)], "w")
    dma("s", lambda: T.sw[:], lambda: T.ws[:], [], [V("sw", 0, 512)], "w")
    dma("s", lambda: T.vt[:], lambda: T.v[:], [], [V("vt", 0, 512)])

    iota(V("uf", 0, 16), [[16, 2], [32, 4], [0, 2]], 0, 0, True)
    iota(V("pi", 0, 2), [[0, 2]], 0, 1, False)
    fill(V("et", 0, 520), 1.0)
    put("g", "sel", lambda: g.affine_select(T.et[:], T.et[:], [[1, 520]], A.is_equal, 0.0, -3, -4),
        [V("et", 0, 520)], [V("et", 0, 520)])
    iota(V("rr", 0, HC), [[0, HC // 32], [1, 32]], 0, 0, True)
    iota(V("r16", 0, HC), [[0, HC // 16], [1, 16]], 0, 0, True)
    iota(tab("cs"), [[32, 10], [0, 2]], 32, 0, True)
    iota(V("sm", 0, 8), [[1, 8]], 0, 0, True)

    def afill(out, c, grp=None):
        af(out, V("zero", 0, out[2]), FN.Identity, 1.0, c, grp=grp)

    def unit(e):
        quant(V("qe", 128 * e, 128), V("se", 128 * e, 128), V("et", 3 - e, 512))

    fill(V("zero", 0, 512), 0.0)
    fill(V("kt", 0, 512), 0.0)
    for a in range(4):
        for p in range(2):
            c = 128 * a + 65 * p
            put("a", "ones", lambda a=a, c=c: act.activation(T.kt[32 * a:32 * a + 32, c:c + 63:2], T.zero[32 * a:32 * a + 32, 0:32],
                                                             FN.Identity, bias=1.0),
                [V("zero", 0, 32)], [V("kt", c, 32, 2)], "kt")
    afill(row("hm"), 1.0)
    afill(row("hi"), 0.0)
    afill(V("hm", 0, 20, 16), 0.0)
    cp(V("uo", 0, 16), V("uf", 0, 16))
    ts(V("qi", 0, 2), V("pi", 0, 2), 15, A.bitwise_and)
    ts(V("ri", 0, 2), V("pi", 0, 2), 31, A.bitwise_and)
    fill(V("rs", 0, HC), HUGE)
    quant(V("ql", 0, 128), V("sl", 0, 128), V("zero", 0, 512))
    cp(col(8), V("qi", 0, 1))
    cp(col(7), V("ri", 0, 1))
    ts(col(6), V("ri", 0, 1), 1 / FRAC - 1, A.mult, -32 / FRAC, A.add)
    fill(V("rs", 0, HC // 32, 32), -HUGE)
    fill(V("cm", 15, 2, 176), -128.0)
    fill(V("rb", RS - 1, 2, RS), 0.0)
    quant(V("qk", 0, 128), V("sk", 0, 128), V("kt", 0, 512))
    quant(V("qu", 0, 128), V("su", 0, 128), V("ut", 0, 512))
    unit(0)
    for p in range(2):
        put("v", "pick", lambda p=p: vec.tensor_copy(T.qp[:, 128 * p:128 * p + 128].bitcast(dt.uint32),
                                                     T.qu[:].bitcast(dt.uint32).indirect(T.uo[:, 8 * p:8 * p + 8])),
            [V("qu", 0, 128), V("uo", 8 * p, 8)], [V("qp", 128 * p, 128)])
        put("a", "pick", lambda p=p: act.activation(T.sp[:, 128 * p:128 * p + 128], T.su[:].indirect(T.uo[:, 8 * p:8 * p + 8]), FN.Copy),
            [V("su", 0, 128), V("uo", 8 * p, 8)], [V("sp", 128 * p, 128)])
        if p == 0:
            quant(half("qx", 0), half("sx", 0), half("xt", 0, 4))
    ts(V("mk", 0, HC), V("rr", 0, HC), col(7), A.not_equal, -HUGE, A.mult)
    for a, cnt, blocks in TILES:
        low = 32 * min(b for b in blocks if b)
        afill(V("ct", 4 * (a + low), 4 * (cnt - low)), 0.0, "ct0")
    af(tab("cs"), tab("cs"), FN.Identity, 1 + 1 / FRAC, col(6))

    def late_constants():
        af(col(1), col(8), FN.Identity, 4.0, 1.0)
        af(col(3), col(8), FN.Identity, OFF1, 0.5 - 15 * OFF1)
        af(col(4), col(8), FN.Identity, -OFF1, 15 * OFF1 - 256.5)
        af(col(5), col(8), FN.Identity, -OFF1, 15 * OFF1 + 128 - 257.0)
        af(col(10), col(8), FN.Identity, OFF2, 4 - 15 * OFF2)
        af(col(11), col(8), FN.Identity, OFF2, 9 - 15 * OFF2)
        af(V("bias", 0, 8), V("sm", 0, 8), FN.Identity, 1.0, col(1))
        af(V("key", C, 4), V("sm", 0, 4), FN.Copy, -1.0)

    def mvi(k):
        return V("mvi", 20 * k, 20)

    later += [
        lambda: unit(1),
        lambda: cp(V("mvo", 0, 60), V("mvi", 0, 60)),
        lambda: tt(three("h1", 1, 0, 20), mvi(1), mvi(0), A.subtract),
        lambda: tt(tab("d2"), mvi(2), mvi(1), A.subtract),
        lambda: unit(2),
        lambda: cp(three("h1", 2, 0, 20), mvi(0)),
        lambda: fill(V("bt", 4 * K, 512 - 4 * K), 0.0),
        lambda: tt(three("h1", 0, 0, 20), tab("d2"), three("h1", 1, 0, 20), A.subtract),
    ]

    n = len(T.cores)
    _, relays, dst = road(T, topo, (rank - 1) % n)
    src_core, in_relays, _ = road(T, topo, rank)
    arrivals = sum(len(topo.engines(c, core)) for c in (in_relays or [src_core, src_core]))
    qk, sk = V("qk", 0, 128), V("sk", 0, 128)
    qv, sv = V("qv", 0, 128), V("sv", 0, 128)
    SV, SA, L0, PV = 0, 2, 4, 7

    def scores(b, n):
        for p in range(2):
            mm(bank(b + p, 0, n), V("qp", 128 * p, 128), V("sp", 128 * p, 128), V("qx", 0, n), V("sx", 0, n))

    def mask(h, b, p):
        tt(V("d1", C * p + HC * h, HC), bank(b + p, HC * h, HC), V("mk", 0, HC), A.add)

    def hold(h, p):
        scan(V("vv", C * p + HC * h, HC), V("rs", 0, HC), V("d1", C * p + HC * h, HC), A.min, A.max)

    def lane(m, p, a=0, step=1, n=None):
        first, cnt, blocks = [t for t in TILES if m in t[2]][0]
        return V("ct", 4 * (first + a) + 2 * blocks.index(m) + p, (n or 32 * m or C) // step, 4 * step)

    def score(m, p):
        return V("vv", C * p + 32 * m + 31, 1)

    def total(m, p, n=1):
        return V("rb", RS * (2 * m + p + 1) - n, n)

    def pack(t):
        a, cnt, blocks = TILES[t]
        quant(V("qc", a, cnt), V("sc", a, cnt), V("ct", 4 * a, 4 * cnt))

    def count(t, r):
        a, cnt, blocks = TILES[t]
        mm(bank(PV, 0, cnt), qk, sk, V("qc", a, cnt), V("sc", a, cnt), t == 0, t == len(TILES) - 1, ("pl", r))

    def arows(rows, b):
        for k in range(len(rows) + 1):
            if k < len(rows):
                m, p = rows[k]
                af(lane(m, p), bank(b + p, 0, 32 * m), FN.Sign, -1.0, score(m, p))
            if k:
                m, p = rows[k - 1]
                af(lane(m, p), lane(m, p), FN.Relu, acc=total(m, p))

    def vrows(rows, b):
        for m, p in rows:
            ts(lane(m, p), bank(b + p, 0, 32 * m), score(m, p), A.is_lt)

    def vsums(rows, r):
        for m, p in rows:
            scan(total(m, p, 16 * m), lane(m, p, 0, 2), lane(m, p, 1, 2), A.add, A.add, grp=("vs", r))

    def inner(h, b, p):
        tt(lane(0, p, HC * h, 1, HC), bank(b + p, HC * h, HC), V("vv", C * p + HC * h, HC), A.is_le)

    def codes_out(q, h):
        dma(q, lambda: T.oc[:, 4 * HC * h:4 * HC * h + 4 * HC], lambda: T.qx[:, HC * h:HC * h + HC].bitcast(dt.uint8),
            [half("qx", h)], [], "o" + q)

    scores(L0, HC)
    scores(L0 + 2, HC)
    quant(half("qx", 1), half("sx", 1), half("xt", 1, 4))
    unit(3)
    mask(0, L0, 0)
    mask(0, L0, 1)
    gap(1)

    for r in range(R):
        last = r == R - 1
        for p in range(2):
            for b in (SV, SA):
                mm(bank(b + p), V("qp", 128 * p, 128), V("sp", 128 * p, 128), row("qx"), row("sx"))
        hold(0, 0)
        hold(0, 1)
        inner(0, L0, 0)
        vrows(VEC_ROWS[0:1], L0)
        arows(ACT_EARLY, L0 + 2)
        vrows(VEC_ROWS[1:2], L0)
        mask(1, SV, 0)
        inner(0, L0, 1)
        vrows(VEC_ROWS[2:3], L0)
        hold(1, 0)
        mask(1, SV, 1)
        vrows(VEC_ROWS[3:4], L0)
        inner(1, SV, 0)
        hold(1, 1)
        vrows(VEC_ROWS[4:5], SV)
        arows(ACT_LATE, SA)
        if r == 0:
            ts(V("r16", 0, HC), V("r16", 0, HC), col(8), A.is_equal)
            for h in range(2):
                af(half("mm", h), V("r16", 0, HC), FN.Identity, 2.0 ** 26, -OFF1)
            late_constants()
        for e in range(3 if r == 0 else 4):
            af(plane("fx", e), V("xn" if r else "xt", e, C, 4), FN.Copy)
        inner(1, SV, 1)
        pack(1)
        for p in range(2):
            scan(V("cm", 176 * p + 16, HC), lane(0, p, 0, 2), lane(0, p, 1, 2), A.add, A.add, -128.0)
        vrows(VEC_ROWS[5:], SV)
        pack(2)
        for p in range(2):
            tt(V("rd", p, 10, 2), V("cm", 176 * p + 15, 10, 16), V("cm", 176 * p + 31, 10, 16), A.subtract, grp=("rd", r))
        vsums(VEC_ROWS[:4], r)
        tt(tab("re"), tab("rd"), tab("cs"), A.add)
        pack(0)
        vsums(VEC_ROWS[4:], r)
        pack(3)
        for t in range(4):
            count(t, r)
        tt(V("hi", 0, 20, 16), tab("re"), V("rb", RS - 1, 20, RS), A.subtract)
        pack(4)
        count(4, r)
        for h in range(2):
            scan(half("hd", h), half("hm", h), half("hi", h), A.mult, A.add)
        gap()
        for h in range(2):
            put("v", "tr", lambda h=h: vec.transpose(ap(half("ov", h)), ap(half("hd", h))), [half("hd", h)], [half("ov", h)])
        gap()

        def sums(m):
            af(V("junk", CW * m, C + 4 - m), row("key", 0, C + 4 - m), FN.Relu, -1.0, V("bias", m, 1), acc=V("gs", m, 1),
               grp=("gs", r))

        for h in range(2):
            tt(half("key", h), bank(PV, HC * h, HC), half("ov", h), A.add)
            af(half("s1", h), half("key", h), FN.Relu, -1024.0, 1024 * 256.5)
        gap()
        scan(half("t1", 0), half("mm", 0), half("key", 0), A.add, A.min)
        gap()
        for h in range(2):
            tt(half("a0", h), half("key", h), half("s1", h), A.min)
        def first_move(a, b, queue):
            off = V("mvo", a // 16, (b - a) // 16)
            if queue == "a":
                af(row("xa", a, b - a), row("a0"), FN.Identity, 1.0, -0.25, off=off)
            else:
                ts(row("xa", a, b - a), row("a0"), -0.25, A.add, off=off)

        def border_list(step):
            if step == 0:
                tt(V("oa", 0, 4), V("gs", 0, 4), V("gs", 1, 4), A.subtract)
            else:
                ts(V("oo", 0, 4), V("oa", 0, 4), FRAC, A.mult)

        def border_tile():
            for e in range(4):
                af(V("bt", e, K, 4), plane("fx", e), FN.Copy, off=V("oo", 0, 4), grp=("bt", r))

        def border_out():
            quant(V("qb", 128 * r, 128), V("sb", 128 * r, 128), V("bt", 0, 512))
            for part in range(2):
                to, where, sem = (dst, "land", "arr%d" % r) if relays is None else (relays[part], "mid", "mid%d" % r)
                put("g", "send", lambda to=to, where=where, sem=sem, part=part, r=r: write(
                    g, T, topo, core, to, piece(T, where, part, r), piece(T, "made", part, r), sem),
                    [V(("qb", "sb")[part], 128 * r, 128)], [])

        soon = r < SOON
        cut = HC if soon else CUT1
        for m in range(5 if soon else 2):
            sums(m)
        if not soon:
            first_move(cut, C, "a")
        af(row("a1"), row("a0"), FN.Identity, 1.0, 0.25)
        for m in range(5 if soon else 2, 5):
            sums(m)
        if r == 0:
            af(plane("fx", 3), V("xt", 3, C, 4), FN.Copy)
            for v, c in ((V("n0", C, 16), 7.0), (V("e1", C, 16), -1.0), (V("c3", C, 16), 15.0)):
                afill(v, c)
        scan(half("t1", 1), half("mm", 1), half("key", 1), A.add, A.min)
        gap()
        if soon:
            first_move(cut, C, "v")
        first_move(0, cut, "v")
        gap()
        for a, b in ((cut, C), (0, cut)):
            link("xb", "a0", "xa", A.min, m1, a, b)
        if soon:
            border_list(0)
        link("c1", "a1", "xb", A.min, m2, cut, C)
        if soon:
            border_list(1)
            border_tile()
        link("c1", "a1", "xb", A.min, m2, 0, cut)
        ts(row("n0", cut, C - cut), row("c1", cut, C - cut), 0.5, A.is_ge, 7.0, A.mult)
        if not soon:
            border_list(0)
        ts(row("n0", 0, cut), row("c1", 0, cut), 0.5, A.is_ge, 7.0, A.mult)
        af(row("ya", CUT2, C - CUT2), row("n0"), FN.Identity, 8.0 / 7, 1.0, off=V("mvo", CUT2 // 16, 20 - CUT2 // 16))
        if not soon:
            border_list(1)
            border_tile()
        scan(row("u1"), row("mm"), row("c1"), A.add, A.min)
        ts(row("ya", 0, CUT2), row("n0"), 8.0 / 7, A.mult, 1.0, A.add, off=V("mvo", 0, CUT2 // 16))
        ts(tab("f1"), ends("u1"), col(3), A.is_lt, float(C), A.mult)
        if soon:
            border_out()
            tt(tab("m2"), tab("f1"), mvi(2), A.max)
        ts(tab("ki"), ends("u1"), 4.0, A.mult, 1.0, A.add)
        gap()
        link("yb", "n0", "ya", A.add, m1, 0, HC)
        if soon:
            cp(m2x, tab("m2"))
        else:
            tt(tab("m2"), tab("f1"), mvi(2), A.max)
        link("yb", "n0", "ya", A.add, m1, HC, C)
        if not soon:
            cp(m2x, tab("m2"))
            border_out()
        af(tab("cb"), ends("t1"), FN.Identity, 1.0, col(5))
        af(tab("sg"), ends("t1"), FN.Sign, 1.0, col(4))
        af(six("g1", 2), tab("cb"), FN.Relu, 1.0, -128.0)
        af(six("g0", 2), tab("sg"), FN.Relu, -1.0, grp=("l0", r))
        af(tab("hb"), six("g1", 2), FN.Identity, 0.25, 159.625)
        af(six("g1", 3), tab("sg"), FN.Relu, float(C), grp=("l0", r))
        af(six("g1", 4), six("g1", 2), FN.Copy, 15.0, grp=("l0", r))
        af(six("g1", 5), tab("hb"), FN.Identity, -63.0, 63.0 * 160, grp=("l0", r))
        if r == 0:
            for h in range(2):
                af(half("m2b", h), V("r16", 0, HC), FN.Identity, 2.0 ** 26, -OFF2)
        for a, b in ((0, HC), (HC, C)):
            link("c2", "n0", "yb", A.max, m2x, a, b)
        af(row("ya", CUT3, C - CUT3), row("c2"), FN.Identity, 1.0, -1.0, off=V("mvo", CUT3 // 16, 20 - CUT3 // 16))
        af(row("e1"), row("c2"), FN.Identity, 1.0, 1.0)
        scan(half("u2", 0), half("m2b", 0), half("c2", 0), A.add, A.min)
        ts(tab("k1"), tab("ki"), 3, A.bitwise_and)
        gap()
        ts(row("ya", 0, CUT3), row("c2"), -1.0, A.add, off=V("mvo", 0, CUT3 // 16))
        scan(half("u2", 1), half("m2b", 1), half("c2", 1), A.add, A.min)
        tt(tab("al"), tab("k1"), tab("f1"), A.subtract)
        gap(2)
        af(tab("kb"), ends("u2"), FN.Relu, -1.0, col(11))
        af(tab("am"), tab("al"), FN.Identity, 1.0, col(10))
        if r == 0:
            afill(three("h0", 0), 0.0)
            af(V("h1", 60, 60), V("h1", 0, 60), FN.Copy)
            for j, c in ((-1, 0.0), (3, 1.0), (4, 1.0), (5, 1.0)):
                afill(six("g0", j), c)
            afill(six("g1", 0), 0.0)
            afill(V("tt", 20, 12), 0.0)
            for e in range(2):
                af(plane("yy", e), V("xt", e, C, 4), FN.Copy, 32.0)
        for a, b in ((0, HC), (HC, C)):
            link("yb", "c2", "ya", A.min, m1, a, b)
        for a, b in ((0, HC), (HC, C)):
            link("c3", "e1", "yb", A.min, m2x, a, b)
        af(row("ya"), row("c3"), FN.Copy, off=m0)
        if CUT4 < C:
            af(row("c4", CUT4, C - CUT4), row("c3", 0, CW), FN.Copy, off=V("m2o", CUT4 // 16, 20 - CUT4 // 16))
        af(row("yc"), row("c3"), FN.Copy, off=m1)
        if r == 0:
            for e in range(2, 4):
                af(plane("yy", e), V("xt", e, C, 4), FN.Copy, 32.0)
        scan(half("u3", 0), half("m2b", 0), half("c3", 0), A.add, A.min)
        cp(tab("zi", 20), tab("kb"))
        scan(half("u3", 1), half("m2b", 1), half("c3", 1), A.add, A.min)
        cp(half("c4", 0), row("c3", 0, CW), off=V("m2o", 0, 10))
        tt(tab("zi"), ends("u3"), tab("am"), A.min)
        cp(row("c4", HC, CUT4 - HC), row("c3", 0, CW), off=V("m2o", 10, (CUT4 - HC) // 16))
        kk = V("kk", 0, 40)
        ts(kk, V("zi", 0, 40), 3, A.bitwise_and)
        scan(row("u6"), row("m2b"), row("ya"), A.add, A.min)
        ts(three("h0", 1), kk, -1.0, A.add, 0.5, A.mult, grp=("kk", r))
        cp(three("h0", 2), kk, grp=("kk", r))
        scan(row("u4"), row("m2b"), row("c4"), A.add, A.min)
        scan(V("ho", 0, 120), V("h0", 0, 120), V("h1", 0, 120), A.mult, A.add)
        scan(row("u5"), row("m2b"), row("yc"), A.add, A.min)
        tt(tab("fl"), ends("u4"), ends("u6"), A.max)
        tt(six("g1", -1), three("ho", 2, 20, 20), three("ho", 2, 0, 20), A.subtract)
        af(six("g1", 1), three("ho", 2, 0, 20), FN.Copy)
        lq, ls = V("ql", K + K * r, 128), V("sl", K + K * r, 128)
        for e in (0, 3, 1, 2):
            mm(bank(L0 + e, 0, 128), V("qe", 128 * e, 128), V("se", 128 * e, 128), lq, ls,
               ext=[("arr%d" % r, arrivals)] if e == 0 else [])
        for e in (0, 3, 1, 2):
            af(plane("fx", e, C, K), bank(L0 + e, K, K), FN.Copy)
        af(V("gw", C, K), bank(L0 + 3, K, K), FN.Copy, 0.5)
        ts(six("g0", 1), ends("u5"), col(10), A.is_lt, grp=("fl", r))
        ts(six("g0", 0), tab("fl"), col(10), A.is_lt, grp=("fl", r))
        scan(V("go", 0, 140), V("g0", 0, 140), V("g1", 0, 140), A.mult, A.add)
        cp(tab("to"), six("go", 5))
        to = tab("to")

        def zrun(e, h):
            return V("zt", e + 2 * C * h, HC, 4)

        for e in range(2):
            af(plane("hh", e, C, K), bank(L0 + e, K, K), FN.Copy, 2.0)
        af(row("gw"), plane("fx", 3, 0, FW), FN.Copy, 0.5, off=to)
        af(plane("hh", 2, C, K), bank(L0 + 2, K, K), FN.Copy, 2.0)
        af(row("gc"), row("gw"), FN.Copy)
        for e in range(3):
            tt(plane("hh", e), plane("fx", e, 0, FW), V("xn" if r else "xt", e, C, 4), A.add, to)
        af(V("zt", 0, C, 4), plane("hh", 0, 0, FW), FN.Copy, 0.5, off=to)
        for e, h in ((1, 0), (1, 1), (2, 1)):
            af(zrun(e, h), plane("hh", e, 0, FW), FN.Copy, 0.5, off=V("to", 10 * h, 10))
        tt(zrun(3, 0), V("gw", 0, FW), half("gc", 0), A.add, V("to", 0, 10))
        ts(zrun(2, 0), plane("hh", 2, 0, FW), 0.5, A.mult, off=V("to", 0, 10))
        tt(V("zt", 3 + 2 * C, 64, 4), V("gw", 0, FW), V("gc", HC, 64), A.add, V("to", 10, 4))
        for h in range(2):
            quant(half("qz", h), half("sz", h), half("zt", h, 4))
            for e in ((0, 1, 2, 3), (3, 0, 1, 2))[h]:
                mm(bank((L0 + e + 4 * h) % 8, 0, HC), V("qw", 128 * e, 128), V("sw", 128 * e, 128), half("qz", h), half("sz", h))
            if h == 0:
                tt(V("zt", 3 + 2 * C + 256, 96, 4), V("gw", 0, FW), V("gc", HC + 64, 96), A.add, V("to", 14, 6))
                if r == 0:
                    quant(qv, sv, V("vt", 0, 512))
                if last:
                    af(V("tt", 0, 20), six("go", 3), FN.Copy)
                    put("v", "tr", lambda: vec.transpose(T.tr[:], T.tt[:]), [V("tt", 0, 32)], [V("tr", 0, 32)])
                    for k in range(8):
                        dma("s", lambda k=k: T.ot[k, :],
                            lambda k=k: T.tr[32 * (k // 2):32 * (k // 2) + 20, 16 * (k % 2):16 * (k % 2) + 16],
                            [V("tr", 0, 32)], [], "ot")
        def add(h, e):
            y = plane("yy", e, HC * h, HC)
            tt(y, bank((L0 + e + 4 * h) % 8, 0, HC), y, A.add)
            if e < 3 and not (last and (h, e) == (1, 2)):
                af(V("xn", 2 * C * h + e, HC, 4), y, FN.Copy, 1.0 / 32, grp=("xn", r, h))

        def cast(h, e=3):
            ts(V("xn", 2 * C * h + e, HC, 4), plane("yy", e, HC * h, HC), 1.0 / 32, A.mult)

        for e in range(4):
            add(0, e)
        add(1, 3)
        cast(0)
        add(1, 0)
        quant(half("qx", 0), half("sx", 0), half("xn", 0, 4))
        if last:
            mm(bank(L0, 0, HC), qv, sv, half("qx", 0), half("sx", 0))
            codes_out("s", 0)
        else:
            scores(L0, HC)
            scores(L0 + 2, HC)
        add(1, 1)
        add(1, 2)
        cast(1)
        if last:
            cast(1, 2)
        else:
            mask(0, L0, 0)
            mask(0, L0, 1)
        quant(half("qx", 1), half("sx", 1), half("xn", 1, 4))

    mm(bank(L0 + 1, 0, HC), qv, sv, half("qx", 1), half("sx", 1))
    af(half("ys", 0), bank(L0, 0, HC), FN.Copy)
    cp(half("ys", 1), bank(L0 + 1, 0, HC))
    dma("s", lambda: T.y[:, 0:HC], lambda: T.ys[:, 0:HC], [half("ys", 0)], [], "os")
    codes_out("a", 1)
    for k in range(4):
        dma("as"[k // 2], lambda k=k: T.osc[4 * k:4 * k + 4, :], lambda k=k: T.sx[32 * k:32 * k + 4, :], [row("sx")], [],
            "o" + "as"[k // 2])
    dma("s", lambda: T.y[:, HC:C], lambda: T.ys[:, HC:C], [half("ys", 1)], [], "os")
    for q in ("s", "a"):
        put(q, "end", None, [], [], after=[i for qq, i in stores if qq == q])
    put("g", "end", None, [], [], ext=[("sent", R * sum(len(topo.engines(core, c)) for c in (relays or [dst, dst])))])
    return ops


def rank_program(g, core, T, topo):
    rank = T.rank_of(core)
    if rank is None:
        for r in range(len(T.cores)):
            src, relays, dst = road(T, topo, r)
            if relays and core in relays:
                relay_program(g, core, T, topo, src, dst, relays.index(core))
        return
    ops = rank_ops(g, core, T, topo, rank)
    run(ops, {"g": g, "v": g.vector, "a": g.scalar, "t": g.tensor, "s": g.sync}, T)
